import numpy as np
import ml_dtypes


def mxq(x, axis, fmt="e4m3"):
    dtype, down = {"e4m3": (ml_dtypes.float8_e4m3fn, 7), "e5m2": (ml_dtypes.float8_e5m2, 14)}[fmt]
    v = np.moveaxis(np.asarray(x, np.float32).astype(ml_dtypes.bfloat16).astype(np.float64), axis, -1)
    blocks = v.reshape(v.shape[:-1] + (-1, 32))
    amax = np.abs(blocks).max(-1, keepdims=True)
    byte = np.maximum(np.where(amax > 0, np.frexp(amax)[1] - 1 + 127, 0) - down, 1)
    scale = np.exp2(byte - 127.0)
    codes = (blocks / scale).astype(np.float32).astype(dtype).astype(np.float64)
    return np.moveaxis((codes * scale).reshape(v.shape), -1, axis)


WIDE = False


def mx_kscale(k):
    if not WIDE:
        return np.ones(k)
    levels = np.array([10, -10, 5, -5, 0])
    if k % 512:
        return np.exp2(np.random.permutation(np.resize(levels, k // 32))).repeat(32)
    a = np.empty((k // 512, 16))
    for p in range(k // 512):
        a[p, :8] = np.random.permutation(np.resize(levels, 8))
        for g in range(8):
            far = levels[np.abs(levels - a[p, g]) >= 10]
            a[p, g + 8] = far[np.random.randint(len(far))]
    return np.exp2(a.ravel()).repeat(32)


def f64(x):
    return np.asarray(x).astype(np.float64)


def striped(idx):
    return np.tile(idx.reshape(-1, 16).T, (8, 1)).astype(np.uint16)


def unstriped(offs):
    return offs[:16].T.reshape(-1).astype(np.int64)


E2M1 = np.array([0.0, 0.5, 1.0, 1.5, 2.0, 3.0, 4.0, 6.0, -0.0, -0.5, -1.0, -1.5, -2.0, -3.0, -4.0, -6.0])


def pack_weight(w, fmt):
    k, n = w.shape
    w = f64(np.asarray(w, np.float32).astype(ml_dtypes.bfloat16)).reshape(k // 32, 32, n)
    amax = np.abs(w).max(1)
    if fmt == "e4m3":
        byte = np.frexp(amax)[1] - 1 + 127 - 7
    else:
        mant, ex = np.frexp(amax / 6.0)
        byte = np.where(mant > 0.5, ex, ex - 1) + 127
    byte = np.clip(np.where(amax > 0, byte, 1), 1, 254)
    scaled = (w * np.exp2(127.0 - byte)[:, None, :]).reshape(k, n).astype(np.float32)
    by_word = np.ascontiguousarray(scaled.reshape(k // 512, 128, 4, n).transpose(0, 1, 3, 2))
    if fmt == "e4m3":
        words = by_word.astype(ml_dtypes.float8_e4m3fn).view(np.uint8)
    else:
        c = by_word.astype(ml_dtypes.float4_e2m1fn).view(np.uint8) & 0xF
        words = (c[..., 0::2] | (c[..., 1::2] << 4)).reshape(k // 512, 128, 2 * n)
    return np.ascontiguousarray(words), np.ascontiguousarray(byte.astype(np.uint8).reshape(k // 512, 16, n))


def unpack_weight(words, scales, fmt):
    g, _, n = scales.shape
    words = np.ascontiguousarray(words).reshape(g, 128, n, -1)
    if fmt == "e4m3":
        vals = words.view(ml_dtypes.float8_e4m3fn).astype(np.float64)
    else:
        nib = np.empty((g, 128, n, 4), np.uint8)
        nib[..., 0::2] = words & 0xF
        nib[..., 1::2] = words >> 4
        vals = E2M1[nib]
    vals = vals * np.repeat(np.exp2(scales.astype(np.float64) - 127.0), 8, axis=1)[..., None]
    return vals.transpose(0, 1, 3, 2).reshape(g * 512, n)


def silu(v):
    return v / (1.0 + np.exp(-np.maximum(v, -700.0)))


K, T, E, C, N = 512, 768, 6, 256, 128


def by_expert(wq, xq):
    return np.concatenate([wq[e].T @ xq[:, e * C:(e + 1) * C] for e in range(E)], axis=1)


def setup_inputs():
    n = np.random.standard_normal
    s = mx_kscale(K)[:, None]
    first = np.random.permutation(np.repeat(np.arange(E), T // E))
    second = (first + 1 + np.random.permutation(np.repeat(np.arange(E - 1), -(-T // (E - 1)))[:T])) % E
    while np.bincount(second, minlength=E).max() != T // E:
        load = np.bincount(second, minlength=E); hi, lo = int(load.argmax()), int(load.argmin())
        t = np.flatnonzero((second == hi) & (first != lo))[0]; second[t] = lo
    slot_token = np.empty(E * C, np.int64); pos = np.empty((2, T), np.int64); fill = np.zeros(E, np.int64)
    place = np.stack([np.random.permutation(C) for _ in range(E)])
    for r, deal in enumerate((first, second)):
        for t in np.random.permutation(T):
            e = deal[t]; j = e * C + place[e, fill[e]]; fill[e] += 1; slot_token[j] = t; pos[r, t] = j
    g = np.random.uniform(0.2, 0.8, T)
    x = pack_weight(n((K, T)) * s, "e4m3")
    return {
        "x_words": x[0],
        "x_scales": x[1],
        "w": (n((E + 1, K, N)) / np.sqrt(K) / s[None]).astype(np.float32),
        "b": (0.3 * n((N, E + 1))).astype(np.float32),
        "gate": np.stack([np.tile(g, (N, 1)), np.tile(1.0 - g, (N, 1))]).astype(np.float32),
        "offs": striped(slot_token),
        "pos1": striped(pos[0]),
        "pos2": striped(pos[1]),
    }


def reference(x_words, x_scales, w, b, gate, offs, pos1, pos2):
    idx = unstriped(offs)
    wq = mxq(f64(w), 1, "e4m3")
    xs = unpack_weight(x_words, x_scales, "e4m3")
    ys = silu((wq[E].T @ xs) + f64(b)[:, E:])
    xq = unpack_weight(x_words, x_scales, "e4m3")[:, idx]
    y = by_expert(wq, xq)
    y = silu(y + np.repeat(f64(b)[:, :E], C, axis=1))
    return ys + f64(gate[0]) * y[:, unstriped(pos1)] + f64(gate[1]) * y[:, unstriped(pos2)]

@@ -1,0 +1,148 @@
+from contextlib import ExitStack
+
+import concourse.mybir as mybir
+
+K, T, E, C, N = 512, 768, 6, 256, 128
+S = E * C
+FLOPS = 2 * K * N * (S + T)
+
+F32 = mybir.dt.float32
+BF16 = mybir.dt.bfloat16
+I32 = mybir.dt.int32
+U32 = mybir.dt.uint32
+U16 = mybir.dt.uint16
+U8 = mybir.dt.uint8
+FP8X4 = mybir.dt.float8_e4m3fn_x4
+SILU = mybir.ActivationFunctionType.Silu
+MULT = mybir.AluOpType.mult
+ADD = mybir.AluOpType.add
+P = 128
+
+
+def tile_moe_shr_lin_silu_kernel(tc, x_words, x_scales, w, b, gate, offs, pos1, pos2, out):
+    nc = tc.nc
+    with ExitStack() as ctx:
+        keep = ctx.enter_context(tc.tile_pool(name="keep", bufs=1))
+        psum = ctx.enter_context(tc.psum_pool(name="psum", bufs=1))
+
+        offs_sb = keep.tile([P, S // 16], U16, name="offs_sb")
+        pos1_sb = keep.tile([P, T // 16], U16, name="pos1_sb")
+        pos2_sb = keep.tile([P, T // 16], U16, name="pos2_sb")
+        xw = keep.tile([P, T], I32, name="xw", align_bytes=64)
+        xs = keep.tile([P, T], U8, name="xs", align_bytes=64)
+        warm_in = keep.tile([P, 1], F32, name="warm_in")
+        warm_out = keep.tile([P, 1], F32, name="warm_out")
+        b_sb = keep.tile([P, E + 1], F32, name="b_sb")
+        gate_sb = [keep.tile([P, T], F32, name=f"gate{r}") for r in range(2)]
+        groups = [(0, 2), (2, 2), (4, 2), (6, 1)]
+        w_raw = [keep.tile([P, n, 4, N], F32, name=f"w_raw{e0}") for e0, n in groups]
+        w_bf = [keep.tile([P, n, N, 4], BF16, name=f"w_bf{e0}", align_bytes=64) for e0, n in groups]
+        w_codes = [keep.tile([P, n * N], U32, name=f"w_codes{e0}", align_bytes=64) for e0, n in groups]
+        w_scales = [keep.tile([P, n * N], U8, name=f"w_scales{e0}", align_bytes=64) for e0, n in groups]
+        gw = keep.tile([P, S], U32, name="gw", align_bytes=64)
+        gs = keep.tile([P, S], U8, name="gs", align_bytes=64)
+        y = keep.tile([P, S], F32, name="y")
+        ys = keep.tile([P, T], F32, name="ys")
+
+        nc.vector.memset(xs[:].bitcast(I32), 0)
+        nc.sync.dma_start(offs_sb[:], offs)
+        nc.sync.dma_start(xw[:], x_words[0].rearrange("p t r -> p (t r)").bitcast(I32))
+        for q in range(4):
+            nc.scalar.dma_start(xs[32 * q : 32 * q + 4, :].bitcast(I32), x_scales[0, 4 * q : 4 * q + 4, :].bitcast(I32))
+        nc.vector.memset(warm_in[:], 0.0)
+        nc.scalar.activation(warm_out[:], warm_in[:], SILU)
+        nc.gpsimd.dma_start(b_sb[:], b)
+        for g, (e0, n) in enumerate(groups):
+            nc.sync.dma_start(
+                w_raw[g][:].rearrange("p e j n -> p e (j n)"),
+                w[e0 : e0 + n].rearrange("e (p j) n -> p e (j n)", j=4),
+            )
+        nc.sync.dma_start(pos1_sb[:], pos1)
+        nc.sync.dma_start(pos2_sb[:], pos2)
+        for r in range(2):
+            nc.sync.dma_start(gate_sb[r][:], gate[r])
+
+        def cast(copy, g, i):
+            copy(
+                w_bf[g][:, i].rearrange("p (c i) j -> p c j i", i=4),
+                w_raw[g][:, i].rearrange("p j (c i) -> p c j i", i=4),
+            )
+
+        def quantize(g):
+            nc.vector.quantize_mx(
+                out=w_codes[g][:].bitcast(FP8X4),
+                scales=w_scales[g][:],
+                in_=w_bf[g][:].rearrange("p e n j -> p (e n j)"),
+            )
+
+        def gather_words(lo, hi):
+            nc.vector.tensor_copy(gw[:, lo:hi], xw[:].bitcast(U32).indirect(offs_sb[:, lo // 16 : hi // 16]))
+
+        def gather_scales(lo, hi):
+            nc.vector.tensor_copy(gs[:, lo:hi], xs[:].indirect(offs_sb[:, lo // 16 : hi // 16]))
+
+        def product(acc, e, words, scales):
+            g, i = divmod(e, 2)
+            nc.tensor.matmul_mx(
+                out=acc,
+                lhsT=w_codes[g][:, i * N : (i + 1) * N].bitcast(FP8X4),
+                lhsT_scale=w_scales[g][:, i * N : (i + 1) * N],
+                rhs=words.bitcast(FP8X4),
+                rhs_scale=scales,
+                start=True,
+                stop=True,
+            )
+
+        def routed(pieces):
+            lo0, hi0 = pieces[0][0], pieces[-1][1]
+            bank = psum.tile([P, hi0 - lo0], F32, name=f"bank{lo0}")
+            for lo, hi in pieces:
+                product(bank[:, lo - lo0 : hi - lo0], lo // C, gw[:, lo:hi], gs[:, lo:hi])
+            for lo, hi in pieces:
+                e = lo // C
+                nc.scalar.activation(y[:, lo:hi], bank[:, lo - lo0 : hi - lo0], SILU, bias=b_sb[:, e : e + 1])
+
+        for g in range(3):
+            for i in range(2):
+                cast(nc.scalar.copy, g, i)
+
+        gather_words(0, 512)
+        for lo in range(0, S, 512):
+            gather_scales(lo, lo + 512)
+        quantize(0)
+        routed([(0, 256), (256, 512)])
+        gather_words(512, 1024)
+        quantize(1)
+        routed([(512, 768), (768, 1024)])
+        gather_words(1024, 1280)
+        quantize(2)
+        routed([(1024, 1280)])
+        gather_words(1280, 1408)
+        routed([(1280, 1408)])
+        gather_words(1408, 1536)
+        routed([(1408, 1536)])
+
+        cast(nc.vector.tensor_copy, 3, 0)
+        quantize(3)
+        for lo, hi in ((0, 512), (512, 768)):
+            bank = psum.tile([P, hi - lo], F32, name=f"shared{lo}")
+            product(bank[:], E, xw[:, lo:hi], xs[:, lo:hi])
+            nc.scalar.activation(ys[:, lo:hi], bank[:], SILU, bias=b_sb[:, E : E + 1])
+
+        first = keep.tile([P, T], F32, name="first")
+        second = keep.tile([P, T], F32, name="second")
+        partial = keep.tile([P, T], F32, name="partial")
+        result = keep.tile([P, T], F32, name="result")
+
+        def gather_second(lo, hi):
+            nc.vector.tensor_tensor(
+                second[:, lo:hi], y[:].indirect(pos2_sb[:, lo // 16 : hi // 16]), gate_sb[1][:, lo:hi], MULT
+            )
+
+        nc.vector.tensor_tensor(first[:], y[:].indirect(pos1_sb[:]), gate_sb[0][:], MULT)
+        gather_second(0, 512)
+        nc.vector.tensor_tensor(partial[:], first[:], ys[:], ADD)
+        gather_second(512, 768)
+        for lo, hi in ((0, 512), (512, 768)):
+            nc.vector.tensor_tensor(result[:, lo:hi], partial[:, lo:hi], second[:, lo:hi], ADD)
+            nc.sync.dma_start(out[:, lo:hi], result[:, lo:hi])

@@ -1,6 +1,7 @@
 from contextlib import ExitStack
 
 import concourse.mybir as mybir
+from concourse.masks import make_identity
 
 K, T, E, C, N = 512, 768, 6, 256, 128
 S = E * C
@@ -35,11 +36,10 @@ def tile_moe_shr_lin_silu_kernel(tc, x_words, x_scales, w, b, gate, offs, pos1, 
         b_sb = keep.tile([P, E + 1], F32, name="b_sb")
         gate_sb = [keep.tile([P, T], F32, name=f"gate{r}") for r in range(2)]
         groups = [(0, 2), (2, 2), (4, 2), (6, 1)]
-        w_raw = [keep.tile([P, n, 4, N], F32, name=f"w_raw{e0}") for e0, n in groups]
+        w_raw = [keep.tile([P, n, 4, N], F32, name=f"w_raw{e0}", tag=f"w_raw{e0}", align_bytes=64) for e0, n in groups]
         w_bf = [keep.tile([P, n, N, 4], BF16, name=f"w_bf{e0}", align_bytes=64) for e0, n in groups]
         w_codes = [keep.tile([P, n * N], U32, name=f"w_codes{e0}", align_bytes=64) for e0, n in groups]
         w_scales = [keep.tile([P, n * N], U8, name=f"w_scales{e0}", align_bytes=64) for e0, n in groups]
-        gw = keep.tile([P, S], U32, name="gw", align_bytes=64)
         gs = keep.tile([P, S], U8, name="gs", align_bytes=64)
         y = keep.tile([P, S], F32, name="y")
         ys = keep.tile([P, T], F32, name="ys")
@@ -51,12 +51,15 @@ def tile_moe_shr_lin_silu_kernel(tc, x_words, x_scales, w, b, gate, offs, pos1, 
             nc.scalar.dma_start(xs[32 * q : 32 * q + 4, :].bitcast(I32), x_scales[0, 4 * q : 4 * q + 4, :].bitcast(I32))
         nc.vector.memset(warm_in[:], 0.0)
         nc.scalar.activation(warm_out[:], warm_in[:], SILU)
-        nc.gpsimd.dma_start(b_sb[:], b)
+        ident = keep.tile([P, P], F32, name="ident")
+        nc.vector.memset(ident[:], 0.0)
+        make_identity(nc, ident[:], nomemset=True)
         for g, (e0, n) in enumerate(groups):
             nc.sync.dma_start(
                 w_raw[g][:].rearrange("p e j n -> p e (j n)"),
                 w[e0 : e0 + n].rearrange("e (p j) n -> p e (j n)", j=4),
             )
+        nc.sync.dma_start(b_sb[:], b)
         nc.sync.dma_start(pos1_sb[:], pos1)
         nc.sync.dma_start(pos2_sb[:], pos2)
         for r in range(2):
@@ -75,8 +78,8 @@ def tile_moe_shr_lin_silu_kernel(tc, x_words, x_scales, w, b, gate, offs, pos1, 
                 in_=w_bf[g][:].rearrange("p e n j -> p (e n j)"),
             )
 
-        def gather_words(lo, hi):
-            nc.vector.tensor_copy(gw[:, lo:hi], xw[:].bitcast(U32).indirect(offs_sb[:, lo // 16 : hi // 16]))
+        def gather_words(dst, lo, hi):
+            nc.vector.tensor_copy(dst, xw[:].bitcast(U32).indirect(offs_sb[:, lo // 16 : hi // 16]))
 
         def gather_scales(lo, hi):
             nc.vector.tensor_copy(gs[:, lo:hi], xs[:].indirect(offs_sb[:, lo // 16 : hi // 16]))
@@ -93,56 +96,78 @@ def tile_moe_shr_lin_silu_kernel(tc, x_words, x_scales, w, b, gate, offs, pos1, 
                 stop=True,
             )
 
-        def routed(pieces):
+        def routed(words, pieces, tag):
             lo0, hi0 = pieces[0][0], pieces[-1][1]
-            bank = psum.tile([P, hi0 - lo0], F32, name=f"bank{lo0}")
+            bank = psum.tile([P, hi0 - lo0], F32, name=f"routed{lo0}", tag=tag)
             for lo, hi in pieces:
-                product(bank[:, lo - lo0 : hi - lo0], lo // C, gw[:, lo:hi], gs[:, lo:hi])
+                product(bank[:, lo - lo0 : hi - lo0], lo // C, words[:, lo - lo0 : hi - lo0], gs[:, lo:hi])
             for lo, hi in pieces:
                 e = lo // C
                 nc.scalar.activation(y[:, lo:hi], bank[:, lo - lo0 : hi - lo0], SILU, bias=b_sb[:, e : e + 1])
 
-        for g in range(3):
-            for i in range(2):
+        for g, (e0, n) in enumerate(groups):
+            for i in range(n):
                 cast(nc.scalar.copy, g, i)
 
-        gather_words(0, 512)
+        words_a = keep.tile([P, 512], U32, name="words_a", align_bytes=64)
+        words_b = keep.tile([P, 512], U32, name="words_b", tag="w_raw2", align_bytes=64)
+        words_c = keep.tile([P, 256], U32, name="words_c", tag="w_raw4", align_bytes=64)
+        words_d = keep.tile([P, 256], U32, name="words_d", tag="w_raw6", align_bytes=64)
+
+        gather_words(words_a[:], 0, 512)
         for lo in range(0, S, 512):
             gather_scales(lo, lo + 512)
         quantize(0)
-        routed([(0, 256), (256, 512)])
-        gather_words(512, 1024)
+        routed(words_a[:], [(0, 256), (256, 512)], "bank0")
+        gather_words(words_b[:], 512, 1024)
         quantize(1)
-        routed([(512, 768), (768, 1024)])
-        gather_words(1024, 1280)
+        routed(words_b[:], [(512, 768), (768, 1024)], "bank1")
+        gather_words(words_c[:], 1024, 1280)
         quantize(2)
-        routed([(1024, 1280)])
-        gather_words(1280, 1408)
-        routed([(1280, 1408)])
-        gather_words(1408, 1536)
-        routed([(1408, 1536)])
-
-        cast(nc.vector.tensor_copy, 3, 0)
+        routed(words_c[:], [(1024, 1280)], "bank2")
+        gather_words(words_d[:, 0:128], 1280, 1408)
+        routed(words_d[:, 0:128], [(1280, 1408)], "bank3")
+        gather_words(words_d[:, 128:256], 1408, 1536)
+        routed(words_d[:, 128:256], [(1408, 1536)], "bank4")
         quantize(3)
-        for lo, hi in ((0, 512), (512, 768)):
-            bank = psum.tile([P, hi - lo], F32, name=f"shared{lo}")
+        for lo, hi, tag in ((0, 256, "bank5"), (256, 512, "bank6"), (512, 768, "bank7")):
+            bank = psum.tile([P, hi - lo], F32, name=f"shared{lo}", tag=tag)
             product(bank[:], E, xw[:, lo:hi], xs[:, lo:hi])
             nc.scalar.activation(ys[:, lo:hi], bank[:], SILU, bias=b_sb[:, E : E + 1])
 
         first = keep.tile([P, T], F32, name="first")
         second = keep.tile([P, T], F32, name="second")
-        partial = keep.tile([P, T], F32, name="partial")
+        turned = keep.tile([P, T], F32, name="turned")
         result = keep.tile([P, T], F32, name="result")
+        W = 256
+        chunks = range(T // W)
 
-        def gather_second(lo, hi):
+        def turn(dst, src, start, stop):
+            nc.tensor.matmul(dst, src, ident[:], start=start, stop=stop, is_transpose=True)
+
+        def fetch(dst, pos_sb, r, c):
+            lo, hi = c * W, (c + 1) * W
             nc.vector.tensor_tensor(
-                second[:, lo:hi], y[:].indirect(pos2_sb[:, lo // 16 : hi // 16]), gate_sb[1][:, lo:hi], MULT
+                dst[:, lo:hi], y[:].indirect(pos_sb[:, lo // 16 : hi // 16]), gate_sb[r][:, lo:hi], MULT
             )
 
-        nc.vector.tensor_tensor(first[:], y[:].indirect(pos1_sb[:]), gate_sb[0][:], MULT)
-        gather_second(0, 512)
-        nc.vector.tensor_tensor(partial[:], first[:], ys[:], ADD)
-        gather_second(512, 768)
-        for lo, hi in ((0, 512), (512, 768)):
-            nc.vector.tensor_tensor(result[:, lo:hi], partial[:, lo:hi], second[:, lo:hi], ADD)
+        sums = [psum.tile([P, W], F32, name=f"sum{c}", tag=f"bank{c}") for c in chunks]
+        back = [psum.tile([P, W], F32, name=f"back{c}", tag=f"bank{3 + c}") for c in chunks]
+        for c in chunks:
+            fetch(first, pos1_sb, 0, c)
+            for h in range(2):
+                lo = c * W + h * P
+                turn(sums[c][:, h * P : (h + 1) * P], ys[:, lo : lo + P], h == 0, False)
+            for h in range(2):
+                lo = c * W + h * P
+                turn(sums[c][:, h * P : (h + 1) * P], first[:, lo : lo + P], False, h == 1)
+            nc.scalar.copy(turned[:, c * W : (c + 1) * W], sums[c][:])
+            for h in range(2):
+                lo = c * W + h * P
+                turn(back[c][:, h * P : (h + 1) * P], turned[:, lo : lo + P], True, True)
+        for c in chunks:
+            fetch(second, pos2_sb, 1, c)
+        for c in chunks:
+            lo, hi = c * W, (c + 1) * W
+            nc.vector.tensor_tensor(result[:, lo:hi], back[c][:], second[:, lo:hi], ADD)
             nc.sync.dma_start(out[:, lo:hi], result[:, lo:hi])

@@ -46,9 +46,8 @@ def tile_moe_shr_lin_silu_kernel(tc, x_words, x_scales, w, b, gate, offs, pos1, 
 
         nc.vector.memset(xs[:].bitcast(I32), 0)
         nc.sync.dma_start(offs_sb[:], offs)
-        nc.sync.dma_start(xw[:], x_words[0].rearrange("p t r -> p (t r)").bitcast(I32))
         for q in range(4):
-            nc.scalar.dma_start(xs[32 * q : 32 * q + 4, :].bitcast(I32), x_scales[0, 4 * q : 4 * q + 4, :].bitcast(I32))
+            (nc.sync if q < 2 else nc.scalar).dma_start(xs[32 * q : 32 * q + 4, :].bitcast(I32), x_scales[0, 4 * q : 4 * q + 4, :].bitcast(I32))
         nc.vector.memset(warm_in[:], 0.0)
         nc.scalar.activation(warm_out[:], warm_in[:], SILU)
         ident = keep.tile([P, P], F32, name="ident")
@@ -59,6 +58,8 @@ def tile_moe_shr_lin_silu_kernel(tc, x_words, x_scales, w, b, gate, offs, pos1, 
                 w_raw[g][:].rearrange("p e j n -> p e (j n)"),
                 w[e0 : e0 + n].rearrange("e (p j) n -> p e (j n)", j=4),
             )
+            if g == 0:
+                nc.sync.dma_start(xw[:], x_words[0].rearrange("p t r -> p (t r)").bitcast(I32))
         nc.sync.dma_start(b_sb[:], b)
         nc.sync.dma_start(pos1_sb[:], pos1)
         nc.sync.dma_start(pos2_sb[:], pos2)
@@ -114,9 +115,9 @@ def tile_moe_shr_lin_silu_kernel(tc, x_words, x_scales, w, b, gate, offs, pos1, 
         words_c = keep.tile([P, 256], U32, name="words_c", tag="w_raw4", align_bytes=64)
         words_d = keep.tile([P, 256], U32, name="words_d", tag="w_raw6", align_bytes=64)
 
-        gather_words(words_a[:], 0, 512)
         for lo in range(0, S, 512):
             gather_scales(lo, lo + 512)
+        gather_words(words_a[:], 0, 512)
         quantize(0)
         routed(words_a[:], [(0, 256), (256, 512)], "bank0")
         gather_words(words_b[:], 512, 1024)

@@ -54,10 +54,12 @@ def tile_moe_shr_lin_silu_kernel(tc, x_words, x_scales, w, b, gate, offs, pos1, 
         nc.vector.memset(ident[:], 0.0)
         make_identity(nc, ident[:], nomemset=True)
         for g, (e0, n) in enumerate(groups):
-            nc.sync.dma_start(
-                w_raw[g][:].rearrange("p e j n -> p e (j n)"),
-                w[e0 : e0 + n].rearrange("e (p j) n -> p e (j n)", j=4),
-            )
+            step = 1 if g == 2 else n
+            for i in range(0, n, step):
+                nc.sync.dma_start(
+                    w_raw[g][:, i : i + step].rearrange("p e j n -> p e (j n)"),
+                    w[e0 + i : e0 + i + step].rearrange("e (p j) n -> p e (j n)", j=4),
+                )
             if g == 0:
                 nc.sync.dma_start(xw[:], x_words[0].rearrange("p t r -> p (t r)").bitcast(I32))
         nc.sync.dma_start(b_sb[:], b)
@@ -140,35 +142,34 @@ def tile_moe_shr_lin_silu_kernel(tc, x_words, x_scales, w, b, gate, offs, pos1, 
         second = keep.tile([P, T], F32, name="second")
         turned = keep.tile([P, T], F32, name="turned")
         result = keep.tile([P, T], F32, name="result")
-        W = 256
-        chunks = range(T // W)
+        chunks = [(0, 384), (384, 640), (640, 768)]
 
-        def turn(dst, src, start, stop):
-            nc.tensor.matmul(dst, src, ident[:], start=start, stop=stop, is_transpose=True)
+        def turn(bank, src, lo, hi, start, stop):
+            for at in range(lo, hi, P):
+                nc.tensor.matmul(
+                    bank[:, at - lo : at - lo + P],
+                    src[:, at : at + P],
+                    ident[:],
+                    start=start and (stop or at == lo),
+                    stop=stop and (start or at + P == hi),
+                    is_transpose=True,
+                )
 
-        def fetch(dst, pos_sb, r, c):
-            lo, hi = c * W, (c + 1) * W
+        def fetch(dst, pos_sb, r, lo, hi):
             nc.vector.tensor_tensor(
                 dst[:, lo:hi], y[:].indirect(pos_sb[:, lo // 16 : hi // 16]), gate_sb[r][:, lo:hi], MULT
             )
 
-        sums = [psum.tile([P, W], F32, name=f"sum{c}", tag=f"bank{c}") for c in chunks]
-        back = [psum.tile([P, W], F32, name=f"back{c}", tag=f"bank{3 + c}") for c in chunks]
-        for c in chunks:
-            fetch(first, pos1_sb, 0, c)
-            for h in range(2):
-                lo = c * W + h * P
-                turn(sums[c][:, h * P : (h + 1) * P], ys[:, lo : lo + P], h == 0, False)
-            for h in range(2):
-                lo = c * W + h * P
-                turn(sums[c][:, h * P : (h + 1) * P], first[:, lo : lo + P], False, h == 1)
-            nc.scalar.copy(turned[:, c * W : (c + 1) * W], sums[c][:])
-            for h in range(2):
-                lo = c * W + h * P
-                turn(back[c][:, h * P : (h + 1) * P], turned[:, lo : lo + P], True, True)
-        for c in chunks:
-            fetch(second, pos2_sb, 1, c)
-        for c in chunks:
-            lo, hi = c * W, (c + 1) * W
+        sums = [psum.tile([P, hi - lo], F32, name=f"sum{c}", tag=f"bank{c}") for c, (lo, hi) in enumerate(chunks)]
+        back = [psum.tile([P, hi - lo], F32, name=f"back{c}", tag=f"bank{3 + c}") for c, (lo, hi) in enumerate(chunks)]
+        for c, (lo, hi) in enumerate(chunks):
+            fetch(first, pos1_sb, 0, lo, hi)
+            turn(sums[c], ys, lo, hi, True, False)
+            turn(sums[c], first, lo, hi, False, True)
+            nc.scalar.copy(turned[:, lo:hi], sums[c][:])
+            turn(back[c], turned, lo, hi, True, True)
+        for lo, hi in chunks:
+            fetch(second, pos2_sb, 1, lo, hi)
+        for c, (lo, hi) in enumerate(chunks):
             nc.vector.tensor_tensor(result[:, lo:hi], back[c][:], second[:, lo:hi], ADD)
             nc.sync.dma_start(out[:, lo:hi], result[:, lo:hi])

@@ -44,14 +44,16 @@ def tile_moe_shr_lin_silu_kernel(tc, x_words, x_scales, w, b, gate, offs, pos1, 
         y = keep.tile([P, S], F32, name="y")
         ys = keep.tile([P, T], F32, name="ys")
 
-        nc.vector.memset(xs[:].bitcast(I32), 0)
+        nc.gpsimd.memset(xs[:].bitcast(I32), 0)
         nc.sync.dma_start(offs_sb[:], offs)
         for q in range(4):
             (nc.sync if q < 2 else nc.scalar).dma_start(xs[32 * q : 32 * q + 4, :].bitcast(I32), x_scales[0, 4 * q : 4 * q + 4, :].bitcast(I32))
-        nc.vector.memset(warm_in[:], 0.0)
+        nc.sync.dma_start(pos1_sb[:], pos1)
+        nc.sync.dma_start(pos2_sb[:], pos2)
+        nc.gpsimd.memset(warm_in[:], 0.0)
         nc.scalar.activation(warm_out[:], warm_in[:], SILU)
         ident = keep.tile([P, P], F32, name="ident")
-        nc.vector.memset(ident[:], 0.0)
+        nc.gpsimd.memset(ident[:], 0.0)
         make_identity(nc, ident[:], nomemset=True)
         for g, (e0, n) in enumerate(groups):
             step = 1 if g == 2 else n
@@ -63,8 +65,6 @@ def tile_moe_shr_lin_silu_kernel(tc, x_words, x_scales, w, b, gate, offs, pos1, 
             if g == 0:
                 nc.sync.dma_start(xw[:], x_words[0].rearrange("p t r -> p (t r)").bitcast(I32))
         nc.sync.dma_start(b_sb[:], b)
-        nc.sync.dma_start(pos1_sb[:], pos1)
-        nc.sync.dma_start(pos2_sb[:], pos2)
         for r in range(2):
             nc.sync.dma_start(gate_sb[r][:], gate[r])
 

@@ -44,10 +44,9 @@ def tile_moe_shr_lin_silu_kernel(tc, x_words, x_scales, w, b, gate, offs, pos1, 
         y = keep.tile([P, S], F32, name="y")
         ys = keep.tile([P, T], F32, name="ys")
 
-        nc.gpsimd.memset(xs[:].bitcast(I32), 0)
         nc.sync.dma_start(offs_sb[:], offs)
         for q in range(4):
-            (nc.sync if q < 2 else nc.scalar).dma_start(xs[32 * q : 32 * q + 4, :].bitcast(I32), x_scales[0, 4 * q : 4 * q + 4, :].bitcast(I32))
+            (nc.sync if q < 2 else nc.scalar).dma_start(xs[32 * q : 32 * q + 32, :].bitcast(I32), x_scales[0, 4 * q : 4 * q + 4, :].bitcast(I32).partition_broadcast(8))
         nc.sync.dma_start(pos1_sb[:], pos1)
         nc.sync.dma_start(pos2_sb[:], pos2)
         nc.gpsimd.memset(warm_in[:], 0.0)
@@ -62,7 +61,7 @@ def tile_moe_shr_lin_silu_kernel(tc, x_words, x_scales, w, b, gate, offs, pos1, 
                     w_raw[g][:, i : i + step].rearrange("p e j n -> p e (j n)"),
                     w[e0 + i : e0 + i + step].rearrange("e (p j) n -> p e (j n)", j=4),
                 )
-            if g == 0:
+            if g == 1:
                 nc.sync.dma_start(xw[:], x_words[0].rearrange("p t r -> p (t r)").bitcast(I32))
         nc.sync.dma_start(b_sb[:], b)
         for r in range(2):
@@ -113,7 +112,7 @@ def tile_moe_shr_lin_silu_kernel(tc, x_words, x_scales, w, b, gate, offs, pos1, 
                 cast(nc.scalar.copy, g, i)
 
         words_a = keep.tile([P, 512], U32, name="words_a", align_bytes=64)
-        words_b = keep.tile([P, 512], U32, name="words_b", tag="w_raw2", align_bytes=64)
+        words_b = keep.tile([P, 512], U32, name="words_b", align_bytes=64)
         words_c = keep.tile([P, 256], U32, name="words_c", tag="w_raw4", align_bytes=64)
         words_d = keep.tile([P, 256], U32, name="words_d", tag="w_raw6", align_bytes=64)
 
@@ -138,17 +137,16 @@ def tile_moe_shr_lin_silu_kernel(tc, x_words, x_scales, w, b, gate, offs, pos1, 
             product(bank[:], E, xw[:, lo:hi], xs[:, lo:hi])
             nc.scalar.activation(ys[:, lo:hi], bank[:], SILU, bias=b_sb[:, E : E + 1])
 
-        first = keep.tile([P, T], F32, name="first")
-        second = keep.tile([P, T], F32, name="second")
+        chunks = [(0, 256), (256, 512), (512, 768)]
+        first = [keep.tile([P, 256], F32, name=f"first{c}", tag=f"first{c}") for c in range(3)]
         turned = keep.tile([P, T], F32, name="turned")
         result = keep.tile([P, T], F32, name="result")
-        chunks = [(0, 384), (384, 640), (640, 768)]
 
         def turn(bank, src, lo, hi, start, stop):
             for at in range(lo, hi, P):
                 nc.tensor.matmul(
                     bank[:, at - lo : at - lo + P],
-                    src[:, at : at + P],
+                    src[:, at - lo : at - lo + P],
                     ident[:],
                     start=start and (stop or at == lo),
                     stop=stop and (start or at + P == hi),
@@ -157,19 +155,40 @@ def tile_moe_shr_lin_silu_kernel(tc, x_words, x_scales, w, b, gate, offs, pos1, 
 
         def fetch(dst, pos_sb, r, lo, hi):
             nc.vector.tensor_tensor(
-                dst[:, lo:hi], y[:].indirect(pos_sb[:, lo // 16 : hi // 16]), gate_sb[r][:, lo:hi], MULT
+                dst, y[:].indirect(pos_sb[:, lo // 16 : hi // 16]), gate_sb[r][:, lo:hi], MULT
             )
 
         sums = [psum.tile([P, hi - lo], F32, name=f"sum{c}", tag=f"bank{c}") for c, (lo, hi) in enumerate(chunks)]
         back = [psum.tile([P, hi - lo], F32, name=f"back{c}", tag=f"bank{3 + c}") for c, (lo, hi) in enumerate(chunks)]
-        for c, (lo, hi) in enumerate(chunks):
-            fetch(first, pos1_sb, 0, lo, hi)
-            turn(sums[c], ys, lo, hi, True, False)
-            turn(sums[c], first, lo, hi, False, True)
+
+        def forth(c):
+            lo, hi = chunks[c]
+            fetch(first[c][:], pos1_sb, 0, lo, hi)
+            turn(sums[c], ys[:, lo:hi], lo, hi, True, False)
+            turn(sums[c], first[c], lo, hi, False, True)
             nc.scalar.copy(turned[:, lo:hi], sums[c][:])
-            turn(back[c], turned, lo, hi, True, True)
-        for lo, hi in chunks:
-            fetch(second, pos2_sb, 1, lo, hi)
-        for c, (lo, hi) in enumerate(chunks):
-            nc.vector.tensor_tensor(result[:, lo:hi], back[c][:], second[:, lo:hi], ADD)
+
+        def turn_back(c):
+            lo, hi = chunks[c]
+            turn(back[c], turned[:, lo:hi], lo, hi, True, True)
+
+        forth(0)
+        forth(1)
+        turn_back(0)
+        forth(2)
+        turn_back(1)
+        turn_back(2)
+        second = keep.tile([P, 512], F32, name="second")
+        second_last = keep.tile([P, 256], F32, name="second_last", tag="first2")
+
+        def finish(c, lo, hi, src):
+            nc.vector.tensor_tensor(result[:, lo:hi], back[c][:, lo - 256 * c : hi - 256 * c], src, ADD)
             nc.sync.dma_start(out[:, lo:hi], result[:, lo:hi])
+
+        fetch(second[:, 0:256], pos2_sb, 1, 0, 256)
+        fetch(second[:, 256:512], pos2_sb, 1, 256, 512)
+        finish(0, 0, 256, second[:, 0:256])
+        fetch(second_last[:], pos2_sb, 1, 512, 768)
+        finish(1, 256, 512, second[:, 256:512])
+        finish(2, 512, 640, second_last[:, 0:128])
+        finish(2, 640, 768, second_last[:, 128:256])

@@ -17,7 +17,14 @@ FP8X4 = mybir.dt.float8_e4m3fn_x4
 SILU = mybir.ActivationFunctionType.Silu
 MULT = mybir.AluOpType.mult
 ADD = mybir.AluOpType.add
+
 P = 128
+PACK = 4
+QUADRANT = 32
+PER_COLUMN = 16
+PAIR = 2 * C
+RANGE = 256
+GROUPS = [(0, 2), (2, 2), (4, 2), (E, 1)]
 
 
 def tile_moe_shr_lin_silu_kernel(tc, x_words, x_scales, w, b, gate, offs, pos1, pos2, out):
@@ -26,27 +33,33 @@ def tile_moe_shr_lin_silu_kernel(tc, x_words, x_scales, w, b, gate, offs, pos1, 
         keep = ctx.enter_context(tc.tile_pool(name="keep", bufs=1))
         psum = ctx.enter_context(tc.psum_pool(name="psum", bufs=1))
 
-        offs_sb = keep.tile([P, S // 16], U16, name="offs_sb")
-        pos1_sb = keep.tile([P, T // 16], U16, name="pos1_sb")
-        pos2_sb = keep.tile([P, T // 16], U16, name="pos2_sb")
-        xw = keep.tile([P, T], I32, name="xw", align_bytes=64)
-        xs = keep.tile([P, T], U8, name="xs", align_bytes=64)
+        offs_sb = keep.tile([P, S // PER_COLUMN], U16, name="offs_sb")
+        pos1_sb = keep.tile([P, T // PER_COLUMN], U16, name="pos1_sb")
+        pos2_sb = keep.tile([P, T // PER_COLUMN], U16, name="pos2_sb")
+        token_words = keep.tile([P, T], I32, name="token_words", align_bytes=64)
+        token_scales = keep.tile([P, T], U8, name="token_scales", align_bytes=64)
         warm_in = keep.tile([P, 1], F32, name="warm_in")
         warm_out = keep.tile([P, 1], F32, name="warm_out")
         b_sb = keep.tile([P, E + 1], F32, name="b_sb")
         gate_sb = [keep.tile([P, T], F32, name=f"gate{r}") for r in range(2)]
-        groups = [(0, 2), (2, 2), (4, 2), (6, 1)]
-        w_raw = [keep.tile([P, n, 4, N], F32, name=f"w_raw{e0}", tag=f"w_raw{e0}", align_bytes=64) for e0, n in groups]
-        w_bf = [keep.tile([P, n, N, 4], BF16, name=f"w_bf{e0}", align_bytes=64) for e0, n in groups]
-        w_codes = [keep.tile([P, n * N], U32, name=f"w_codes{e0}", align_bytes=64) for e0, n in groups]
-        w_scales = [keep.tile([P, n * N], U8, name=f"w_scales{e0}", align_bytes=64) for e0, n in groups]
-        gs = keep.tile([P, S], U8, name="gs", align_bytes=64)
+        w_raw = [
+            keep.tile([P, n, PACK, N], F32, name=f"w_raw{e0}", tag=f"w_raw{e0}", align_bytes=64) for e0, n in GROUPS
+        ]
+        w_bf = [keep.tile([P, n, N, PACK], BF16, name=f"w_bf{e0}", align_bytes=64) for e0, n in GROUPS]
+        w_codes = [keep.tile([P, n * N], U32, name=f"w_codes{e0}", align_bytes=64) for e0, n in GROUPS]
+        w_scales = [keep.tile([P, n * N], U8, name=f"w_scales{e0}", align_bytes=64) for e0, n in GROUPS]
+        slot_scales = keep.tile([P, S], U8, name="slot_scales", align_bytes=64)
         y = keep.tile([P, S], F32, name="y")
         ys = keep.tile([P, T], F32, name="ys")
 
+        nc.gpsimd.memset(token_scales[:].bitcast(I32), 0)
         nc.sync.dma_start(offs_sb[:], offs)
-        for q in range(4):
-            (nc.sync if q < 2 else nc.scalar).dma_start(xs[32 * q : 32 * q + 32, :].bitcast(I32), x_scales[0, 4 * q : 4 * q + 4, :].bitcast(I32).partition_broadcast(8))
+        for q in range(P // QUADRANT):
+            queue = nc.sync if q < 2 else nc.scalar
+            queue.dma_start(
+                token_scales[QUADRANT * q : QUADRANT * q + PACK, :].bitcast(I32),
+                x_scales[0, PACK * q : PACK * q + PACK, :].bitcast(I32),
+            )
         nc.sync.dma_start(pos1_sb[:], pos1)
         nc.sync.dma_start(pos2_sb[:], pos2)
         nc.gpsimd.memset(warm_in[:], 0.0)
@@ -54,24 +67,30 @@ def tile_moe_shr_lin_silu_kernel(tc, x_words, x_scales, w, b, gate, offs, pos1, 
         ident = keep.tile([P, P], F32, name="ident")
         nc.gpsimd.memset(ident[:], 0.0)
         make_identity(nc, ident[:], nomemset=True)
-        for g, (e0, n) in enumerate(groups):
-            step = 1 if g == 2 else n
-            for i in range(0, n, step):
-                nc.sync.dma_start(
-                    w_raw[g][:, i : i + step].rearrange("p e j n -> p e (j n)"),
-                    w[e0 + i : e0 + i + step].rearrange("e (p j) n -> p e (j n)", j=4),
-                )
-            if g == 1:
-                nc.sync.dma_start(xw[:], x_words[0].rearrange("p t r -> p (t r)").bitcast(I32))
+
+        def load_weights(g, first, count):
+            e = GROUPS[g][0] + first
+            nc.sync.dma_start(
+                w_raw[g][:, first : first + count].rearrange("p e j n -> p e (j n)"),
+                w[e : e + count].rearrange("e (p j) n -> p e (j n)", j=PACK),
+            )
+
+        load_weights(0, 0, 2)
+        load_weights(1, 0, 2)
+        nc.sync.dma_start(token_words[:], x_words[0].rearrange("p t r -> p (t r)").bitcast(I32))
+        load_weights(2, 0, 1)
+        load_weights(2, 1, 1)
+        load_weights(3, 0, 1)
         nc.sync.dma_start(b_sb[:], b)
         for r in range(2):
             nc.sync.dma_start(gate_sb[r][:], gate[r])
 
-        def cast(copy, g, i):
-            copy(
-                w_bf[g][:, i].rearrange("p (c i) j -> p c j i", i=4),
-                w_raw[g][:, i].rearrange("p j (c i) -> p c j i", i=4),
-            )
+        for g, (e0, n) in enumerate(GROUPS):
+            for i in range(n):
+                nc.scalar.copy(
+                    w_bf[g][:, i].rearrange("p (c i) j -> p c j i", i=4),
+                    w_raw[g][:, i].rearrange("p j (c i) -> p c j i", i=4),
+                )
 
         def quantize(g):
             nc.vector.quantize_mx(
@@ -80,11 +99,11 @@ def tile_moe_shr_lin_silu_kernel(tc, x_words, x_scales, w, b, gate, offs, pos1, 
                 in_=w_bf[g][:].rearrange("p e n j -> p (e n j)"),
             )
 
-        def gather_words(dst, lo, hi):
-            nc.vector.tensor_copy(dst, xw[:].bitcast(U32).indirect(offs_sb[:, lo // 16 : hi // 16]))
+        def entries(list_sb, lo, hi):
+            return list_sb[:, lo // PER_COLUMN : hi // PER_COLUMN]
 
-        def gather_scales(lo, hi):
-            nc.vector.tensor_copy(gs[:, lo:hi], xs[:].indirect(offs_sb[:, lo // 16 : hi // 16]))
+        def gather_words(dst, lo, hi):
+            nc.vector.tensor_copy(dst, token_words[:].bitcast(U32).indirect(entries(offs_sb, lo, hi)))
 
         def product(acc, e, words, scales):
             g, i = divmod(e, 2)
@@ -98,97 +117,87 @@ def tile_moe_shr_lin_silu_kernel(tc, x_words, x_scales, w, b, gate, offs, pos1, 
                 stop=True,
             )
 
-        def routed(words, pieces, tag):
-            lo0, hi0 = pieces[0][0], pieces[-1][1]
+        def routed(words, lo0, hi0, tag):
             bank = psum.tile([P, hi0 - lo0], F32, name=f"routed{lo0}", tag=tag)
+            pieces = [(lo, min(lo + C, hi0)) for lo in range(lo0, hi0, C)]
             for lo, hi in pieces:
-                product(bank[:, lo - lo0 : hi - lo0], lo // C, words[:, lo - lo0 : hi - lo0], gs[:, lo:hi])
+                product(bank[:, lo - lo0 : hi - lo0], lo // C, words[:, lo - lo0 : hi - lo0], slot_scales[:, lo:hi])
             for lo, hi in pieces:
                 e = lo // C
                 nc.scalar.activation(y[:, lo:hi], bank[:, lo - lo0 : hi - lo0], SILU, bias=b_sb[:, e : e + 1])
 
-        for g, (e0, n) in enumerate(groups):
-            for i in range(n):
-                cast(nc.scalar.copy, g, i)
+        words01 = keep.tile([P, PAIR], U32, name="words01", align_bytes=64)
+        words23 = keep.tile([P, PAIR], U32, name="words23", align_bytes=64)
+        words4 = keep.tile([P, C], U32, name="words4", tag="w_raw4", align_bytes=64)
+        words5 = keep.tile([P, C], U32, name="words5", tag=f"w_raw{E}", align_bytes=64)
 
-        words_a = keep.tile([P, 512], U32, name="words_a", align_bytes=64)
-        words_b = keep.tile([P, 512], U32, name="words_b", align_bytes=64)
-        words_c = keep.tile([P, 256], U32, name="words_c", tag="w_raw4", align_bytes=64)
-        words_d = keep.tile([P, 256], U32, name="words_d", tag="w_raw6", align_bytes=64)
-
-        for lo in range(0, S, 512):
-            gather_scales(lo, lo + 512)
-        gather_words(words_a[:], 0, 512)
-        quantize(0)
-        routed(words_a[:], [(0, 256), (256, 512)], "bank0")
-        gather_words(words_b[:], 512, 1024)
-        quantize(1)
-        routed(words_b[:], [(512, 768), (768, 1024)], "bank1")
-        gather_words(words_c[:], 1024, 1280)
+        for lo in range(0, S, PAIR):
+            nc.vector.tensor_copy(
+                slot_scales[:, lo : lo + PAIR], token_scales[:].indirect(entries(offs_sb, lo, lo + PAIR))
+            )
+        for g, words in enumerate((words01, words23)):
+            gather_words(words[:], g * PAIR, (g + 1) * PAIR)
+            quantize(g)
+            routed(words[:], g * PAIR, (g + 1) * PAIR, f"bank{g}")
+        gather_words(words4[:], 4 * C, 5 * C)
         quantize(2)
-        routed(words_c[:], [(1024, 1280)], "bank2")
-        gather_words(words_d[:, 0:128], 1280, 1408)
-        routed(words_d[:, 0:128], [(1280, 1408)], "bank3")
-        gather_words(words_d[:, 128:256], 1408, 1536)
-        routed(words_d[:, 128:256], [(1408, 1536)], "bank4")
+        routed(words4[:], 4 * C, 5 * C, "bank2")
+        for h in range(2):
+            lo = 5 * C + h * P
+            gather_words(words5[:, h * P : (h + 1) * P], lo, lo + P)
+            routed(words5[:, h * P : (h + 1) * P], lo, lo + P, f"bank{3 + h}")
         quantize(3)
-        for lo, hi, tag in ((0, 256, "bank5"), (256, 512, "bank6"), (512, 768, "bank7")):
-            bank = psum.tile([P, hi - lo], F32, name=f"shared{lo}", tag=tag)
-            product(bank[:], E, xw[:, lo:hi], xs[:, lo:hi])
+        ranges = [(lo, lo + RANGE) for lo in range(0, T, RANGE)]
+        for c, (lo, hi) in enumerate(ranges):
+            bank = psum.tile([P, RANGE], F32, name=f"shared{lo}", tag=f"bank{5 + c}")
+            product(bank[:], E, token_words[:, lo:hi], token_scales[:, lo:hi])
             nc.scalar.activation(ys[:, lo:hi], bank[:], SILU, bias=b_sb[:, E : E + 1])
 
-        chunks = [(0, 256), (256, 512), (512, 768)]
-        first = [keep.tile([P, 256], F32, name=f"first{c}", tag=f"first{c}") for c in range(3)]
+        first = [keep.tile([P, RANGE], F32, name=f"first{c}", tag=f"first{c}") for c in range(len(ranges))]
         turned = keep.tile([P, T], F32, name="turned")
         result = keep.tile([P, T], F32, name="result")
+        sums = [psum.tile([P, RANGE], F32, name=f"sum{c}", tag=f"bank{c}") for c in range(len(ranges))]
+        back = [psum.tile([P, RANGE], F32, name=f"back{c}", tag=f"bank{3 + c}") for c in range(len(ranges))]
 
-        def turn(bank, src, lo, hi, start, stop):
-            for at in range(lo, hi, P):
+        def turn(bank, src, opens, closes):
+            for at in range(0, RANGE, P):
                 nc.tensor.matmul(
-                    bank[:, at - lo : at - lo + P],
-                    src[:, at - lo : at - lo + P],
+                    bank[:, at : at + P],
+                    src[:, at : at + P],
                     ident[:],
-                    start=start and (stop or at == lo),
-                    stop=stop and (start or at + P == hi),
+                    start=opens and (closes or at == 0),
+                    stop=closes and (opens or at + P == RANGE),
                     is_transpose=True,
                 )
 
         def fetch(dst, pos_sb, r, lo, hi):
-            nc.vector.tensor_tensor(
-                dst, y[:].indirect(pos_sb[:, lo // 16 : hi // 16]), gate_sb[r][:, lo:hi], MULT
-            )
-
-        sums = [psum.tile([P, hi - lo], F32, name=f"sum{c}", tag=f"bank{c}") for c, (lo, hi) in enumerate(chunks)]
-        back = [psum.tile([P, hi - lo], F32, name=f"back{c}", tag=f"bank{3 + c}") for c, (lo, hi) in enumerate(chunks)]
-
-        def forth(c):
-            lo, hi = chunks[c]
-            fetch(first[c][:], pos1_sb, 0, lo, hi)
-            turn(sums[c], ys[:, lo:hi], lo, hi, True, False)
-            turn(sums[c], first[c], lo, hi, False, True)
-            nc.scalar.copy(turned[:, lo:hi], sums[c][:])
+            nc.vector.tensor_tensor(dst, y[:].indirect(entries(pos_sb, lo, hi)), gate_sb[r][:, lo:hi], MULT)
 
         def turn_back(c):
-            lo, hi = chunks[c]
-            turn(back[c], turned[:, lo:hi], lo, hi, True, True)
+            lo, hi = ranges[c]
+            turn(back[c], turned[:, lo:hi], True, True)
 
-        forth(0)
-        forth(1)
-        turn_back(0)
-        forth(2)
-        turn_back(1)
-        turn_back(2)
-        second = keep.tile([P, 512], F32, name="second")
-        second_last = keep.tile([P, 256], F32, name="second_last", tag="first2")
+        for c, (lo, hi) in enumerate(ranges):
+            fetch(first[c][:], pos1_sb, 0, lo, hi)
+            turn(sums[c], ys[:, lo:hi], True, False)
+            turn(sums[c], first[c], False, True)
+            nc.scalar.copy(turned[:, lo:hi], sums[c][:])
+            if c > 0:
+                turn_back(c - 1)
+        turn_back(len(ranges) - 1)
 
-        def finish(c, lo, hi, src):
-            nc.vector.tensor_tensor(result[:, lo:hi], back[c][:, lo - 256 * c : hi - 256 * c], src, ADD)
+        second = keep.tile([P, 2 * RANGE], F32, name="second")
+        second_last = keep.tile([P, RANGE], F32, name="second_last", tag="first2")
+
+        def finish(lo, hi, second_part):
+            c, at = divmod(lo, RANGE)
+            nc.vector.tensor_tensor(result[:, lo:hi], back[c][:, at : at + hi - lo], second_part, ADD)
             nc.sync.dma_start(out[:, lo:hi], result[:, lo:hi])
 
-        fetch(second[:, 0:256], pos2_sb, 1, 0, 256)
-        fetch(second[:, 256:512], pos2_sb, 1, 256, 512)
-        finish(0, 0, 256, second[:, 0:256])
-        fetch(second_last[:], pos2_sb, 1, 512, 768)
-        finish(1, 256, 512, second[:, 256:512])
-        finish(2, 512, 640, second_last[:, 0:128])
-        finish(2, 640, 768, second_last[:, 128:256])
+        for lo, hi in ranges[:2]:
+            fetch(second[:, lo:hi], pos2_sb, 1, lo, hi)
+        finish(0, RANGE, second[:, 0:RANGE])
+        fetch(second_last[:], pos2_sb, 1, 2 * RANGE, T)
+        finish(RANGE, 2 * RANGE, second[:, RANGE : 2 * RANGE])
+        for at in range(0, RANGE, P):
+            finish(2 * RANGE + at, 2 * RANGE + at + P, second_last[:, at : at + P])

@@ -25,6 +25,7 @@ PER_COLUMN = 16
 PAIR = 2 * C
 RANGE = 256
 GROUPS = [(0, 2), (2, 2), (4, 2), (E, 1)]
+LOADS = [(0, 1), (1, 2), (3, 1), (4, 1), (5, 1), (E, 1)]
 
 
 def tile_moe_shr_lin_silu_kernel(tc, x_words, x_scales, w, b, gate, offs, pos1, pos2, out):
@@ -43,7 +44,7 @@ def tile_moe_shr_lin_silu_kernel(tc, x_words, x_scales, w, b, gate, offs, pos1, 
         b_sb = keep.tile([P, E + 1], F32, name="b_sb")
         gate_sb = [keep.tile([P, T], F32, name=f"gate{r}") for r in range(2)]
         w_raw = [
-            keep.tile([P, n, PACK, N], F32, name=f"w_raw{e0}", tag=f"w_raw{e0}", align_bytes=64) for e0, n in GROUPS
+            keep.tile([P, n, PACK, N], F32, name=f"w_raw{e0}", tag=f"w_raw{e0}", align_bytes=64) for e0, n in LOADS
         ]
         w_bf = [keep.tile([P, n, N, PACK], BF16, name=f"w_bf{e0}", align_bytes=64) for e0, n in GROUPS]
         w_codes = [keep.tile([P, n * N], U32, name=f"w_codes{e0}", align_bytes=64) for e0, n in GROUPS]
@@ -61,34 +62,33 @@ def tile_moe_shr_lin_silu_kernel(tc, x_words, x_scales, w, b, gate, offs, pos1, 
                 x_scales[0, PACK * q : PACK * q + PACK, :].bitcast(I32),
             )
         nc.sync.dma_start(pos1_sb[:], pos1)
-        nc.sync.dma_start(pos2_sb[:], pos2)
         nc.gpsimd.memset(warm_in[:], 0.0)
         nc.scalar.activation(warm_out[:], warm_in[:], SILU)
         ident = keep.tile([P, P], F32, name="ident")
         nc.gpsimd.memset(ident[:], 0.0)
         make_identity(nc, ident[:], nomemset=True)
 
-        def load_weights(g, first, count):
-            e = GROUPS[g][0] + first
+        def load_weights(g):
+            e, count = LOADS[g]
             nc.sync.dma_start(
-                w_raw[g][:, first : first + count].rearrange("p e j n -> p e (j n)"),
+                w_raw[g][:].rearrange("p e j n -> p e (j n)"),
                 w[e : e + count].rearrange("e (p j) n -> p e (j n)", j=PACK),
             )
 
-        load_weights(0, 0, 2)
-        load_weights(1, 0, 2)
+        load_weights(0)
+        load_weights(1)
         nc.sync.dma_start(token_words[:], x_words[0].rearrange("p t r -> p (t r)").bitcast(I32))
-        load_weights(2, 0, 1)
-        load_weights(2, 1, 1)
-        load_weights(3, 0, 1)
+        for g in range(2, len(LOADS)):
+            load_weights(g)
         nc.sync.dma_start(b_sb[:], b)
+        nc.sync.dma_start(pos2_sb[:], pos2)
         for r in range(2):
             nc.sync.dma_start(gate_sb[r][:], gate[r])
 
-        for g, (e0, n) in enumerate(GROUPS):
+        for g, (e0, n) in enumerate(LOADS):
             for i in range(n):
                 nc.scalar.copy(
-                    w_bf[g][:, i].rearrange("p (c i) j -> p c j i", i=4),
+                    w_bf[(e0 + i) // 2][:, (e0 + i) % 2].rearrange("p (c i) j -> p c j i", i=4),
                     w_raw[g][:, i].rearrange("p j (c i) -> p c j i", i=4),
                 )
 
@@ -128,7 +128,7 @@ def tile_moe_shr_lin_silu_kernel(tc, x_words, x_scales, w, b, gate, offs, pos1, 
 
         words01 = keep.tile([P, PAIR], U32, name="words01", align_bytes=64)
         words23 = keep.tile([P, PAIR], U32, name="words23", align_bytes=64)
-        words4 = keep.tile([P, C], U32, name="words4", tag="w_raw4", align_bytes=64)
+        words4 = keep.tile([P, C], U32, name="words4", tag="w_raw5", align_bytes=64)
         words5 = keep.tile([P, C], U32, name="words5", tag=f"w_raw{E}", align_bytes=64)
 
         for lo in range(0, S, PAIR):

@@ -23,8 +23,10 @@ PACK = 4
 QUADRANT = 32
 PER_COLUMN = 16
 PAIR = 2 * C
+SCALE_WINDOW = 2048
+WORD_WINDOW = 1024
 RANGE = 256
-GROUPS = [(0, 2), (2, 2), (4, 2), (E, 1)]
+GROUPS = [(0, 4), (4, 2), (E, 1)]
 LOADS = [(0, 1), (1, 2), (3, 1), (4, 1), (5, 1), (E, 1)]
 
 
@@ -37,8 +39,8 @@ def tile_moe_shr_lin_silu_kernel(tc, x_words, x_scales, w, b, gate, offs, pos1, 
         offs_sb = keep.tile([P, S // PER_COLUMN], U16, name="offs_sb")
         pos1_sb = keep.tile([P, T // PER_COLUMN], U16, name="pos1_sb")
         pos2_sb = keep.tile([P, T // PER_COLUMN], U16, name="pos2_sb")
-        token_words = keep.tile([P, T], I32, name="token_words", align_bytes=64)
-        token_scales = keep.tile([P, T], U8, name="token_scales", align_bytes=64)
+        token_words = keep.tile([P, WORD_WINDOW], I32, name="token_words", align_bytes=64)
+        token_scales = keep.tile([P, SCALE_WINDOW], U8, name="token_scales", align_bytes=64)
         warm_in = keep.tile([P, 1], F32, name="warm_in")
         warm_out = keep.tile([P, 1], F32, name="warm_out")
         b_sb = keep.tile([P, E + 1], F32, name="b_sb")
@@ -53,16 +55,18 @@ def tile_moe_shr_lin_silu_kernel(tc, x_words, x_scales, w, b, gate, offs, pos1, 
         y = keep.tile([P, S], F32, name="y")
         ys = keep.tile([P, T], F32, name="ys")
 
-        nc.gpsimd.memset(token_scales[:].bitcast(I32), 0)
+        nc.gpsimd.memset(token_scales[:, :T].bitcast(I32), 0)
         nc.sync.dma_start(offs_sb[:], offs)
         for q in range(P // QUADRANT):
             queue = nc.sync if q < 2 else nc.scalar
             queue.dma_start(
-                token_scales[QUADRANT * q : QUADRANT * q + PACK, :].bitcast(I32),
+                token_scales[QUADRANT * q : QUADRANT * q + PACK, :T].bitcast(I32),
                 x_scales[0, PACK * q : PACK * q + PACK, :].bitcast(I32),
             )
         nc.sync.dma_start(pos1_sb[:], pos1)
         nc.gpsimd.memset(warm_in[:], 0.0)
+        nc.gpsimd.memset(token_scales[:, T:].bitcast(I32), 0)
+        nc.gpsimd.memset(token_words[:, T:], 0)
         nc.scalar.activation(warm_out[:], warm_in[:], SILU)
         ident = keep.tile([P, P], F32, name="ident")
         nc.gpsimd.memset(ident[:], 0.0)
@@ -77,7 +81,7 @@ def tile_moe_shr_lin_silu_kernel(tc, x_words, x_scales, w, b, gate, offs, pos1, 
 
         load_weights(0)
         load_weights(1)
-        nc.sync.dma_start(token_words[:], x_words[0].rearrange("p t r -> p (t r)").bitcast(I32))
+        nc.sync.dma_start(token_words[:, :T], x_words[0].rearrange("p t r -> p (t r)").bitcast(I32))
         for g in range(2, len(LOADS)):
             load_weights(g)
         nc.sync.dma_start(b_sb[:], b)
@@ -85,10 +89,11 @@ def tile_moe_shr_lin_silu_kernel(tc, x_words, x_scales, w, b, gate, offs, pos1, 
         for r in range(2):
             nc.sync.dma_start(gate_sb[r][:], gate[r])
 
+        group_of = {e0 + i: (g, i) for g, (e0, n) in enumerate(GROUPS) for i in range(n)}
         for g, (e0, n) in enumerate(LOADS):
             for i in range(n):
                 nc.scalar.copy(
-                    w_bf[(e0 + i) // 2][:, (e0 + i) % 2].rearrange("p (c i) j -> p c j i", i=4),
+                    w_bf[group_of[e0 + i][0]][:, group_of[e0 + i][1]].rearrange("p (c i) j -> p c j i", i=4),
                     w_raw[g][:, i].rearrange("p j (c i) -> p c j i", i=4),
                 )
 
@@ -103,10 +108,11 @@ def tile_moe_shr_lin_silu_kernel(tc, x_words, x_scales, w, b, gate, offs, pos1, 
             return list_sb[:, lo // PER_COLUMN : hi // PER_COLUMN]
 
         def gather_words(dst, lo, hi):
-            nc.vector.tensor_copy(dst, token_words[:].bitcast(U32).indirect(entries(offs_sb, lo, hi)))
+            window = token_words[:] if hi - lo >= T else token_words[:, :T]
+            nc.vector.tensor_copy(dst, window.bitcast(U32).indirect(entries(offs_sb, lo, hi)))
 
         def product(acc, e, words, scales):
-            g, i = divmod(e, 2)
+            g, i = group_of[e]
             nc.tensor.matmul_mx(
                 out=acc,
                 lhsT=w_codes[g][:, i * N : (i + 1) * N].bitcast(FP8X4),
@@ -117,47 +123,44 @@ def tile_moe_shr_lin_silu_kernel(tc, x_words, x_scales, w, b, gate, offs, pos1, 
                 stop=True,
             )
 
-        def routed(words, lo0, hi0, tag):
-            bank = psum.tile([P, hi0 - lo0], F32, name=f"routed{lo0}", tag=tag)
-            pieces = [(lo, min(lo + C, hi0)) for lo in range(lo0, hi0, C)]
-            for lo, hi in pieces:
-                product(bank[:, lo - lo0 : hi - lo0], lo // C, words[:, lo - lo0 : hi - lo0], slot_scales[:, lo:hi])
-            for lo, hi in pieces:
+        def routed(words, base, lo0, hi0):
+            cuts = sorted({lo0, hi0} | set(range(-(-lo0 // C) * C, hi0, C)))
+            for lo, hi in zip(cuts, cuts[1:]):
                 e = lo // C
-                nc.scalar.activation(y[:, lo:hi], bank[:, lo - lo0 : hi - lo0], SILU, bias=b_sb[:, e : e + 1])
+                bank = psum.tile([P, hi - lo], F32, name=f"routed{lo}", tag=f"bank{len(used) % 8}")
+                used.append(lo)
+                product(bank[:], e, words[:, lo - base : hi - base], slot_scales[:, lo:hi])
+                nc.scalar.activation(y[:, lo:hi], bank[:], SILU, bias=b_sb[:, e : e + 1])
 
-        words01 = keep.tile([P, PAIR], U32, name="words01", align_bytes=64)
-        words23 = keep.tile([P, PAIR], U32, name="words23", align_bytes=64)
-        words4 = keep.tile([P, C], U32, name="words4", tag="w_raw5", align_bytes=64)
-        words5 = keep.tile([P, C], U32, name="words5", tag=f"w_raw{E}", align_bytes=64)
+        used = []
+        words_a = keep.tile([P, 3 * C], U32, name="words_a", align_bytes=64)
+        words_b = keep.tile([P, 3 * P], U32, name="words_b", tag="w_raw4", align_bytes=64)
+        words_c = keep.tile([P, 3 * P], U32, name="words_c", tag="w_raw5", align_bytes=64)
 
-        for lo in range(0, S, PAIR):
-            nc.vector.tensor_copy(
-                slot_scales[:, lo : lo + PAIR], token_scales[:].indirect(entries(offs_sb, lo, lo + PAIR))
-            )
-        for g, words in enumerate((words01, words23)):
-            gather_words(words[:], g * PAIR, (g + 1) * PAIR)
-            quantize(g)
-            routed(words[:], g * PAIR, (g + 1) * PAIR, f"bank{g}")
-        gather_words(words4[:], 4 * C, 5 * C)
+        nc.vector.tensor_copy(slot_scales[:], token_scales[:].indirect(offs_sb[:]))
+        gather_words(words_a[:], 0, 6 * P)
+        quantize(0)
+        routed(words_a, 0, 0, 6 * P)
+        gather_words(words_b[:], 6 * P, 9 * P)
+        routed(words_b, 6 * P, 6 * P, 8 * P)
+        quantize(1)
+        routed(words_b, 6 * P, 8 * P, 9 * P)
+        gather_words(words_c[:, : 2 * P], 9 * P, 11 * P)
+        routed(words_c, 9 * P, 9 * P, 11 * P)
+        gather_words(words_c[:, 2 * P :], 11 * P, S)
+        routed(words_c, 9 * P, 11 * P, S)
         quantize(2)
-        routed(words4[:], 4 * C, 5 * C, "bank2")
-        for h in range(2):
-            lo = 5 * C + h * P
-            gather_words(words5[:, h * P : (h + 1) * P], lo, lo + P)
-            routed(words5[:, h * P : (h + 1) * P], lo, lo + P, f"bank{3 + h}")
-        quantize(3)
         ranges = [(lo, lo + RANGE) for lo in range(0, T, RANGE)]
         for c, (lo, hi) in enumerate(ranges):
-            bank = psum.tile([P, RANGE], F32, name=f"shared{lo}", tag=f"bank{5 + c}")
+            bank = psum.tile([P, RANGE], F32, name=f"shared{lo}", tag=f"bank{c}")
             product(bank[:], E, token_words[:, lo:hi], token_scales[:, lo:hi])
             nc.scalar.activation(ys[:, lo:hi], bank[:], SILU, bias=b_sb[:, E : E + 1])
 
-        first = [keep.tile([P, RANGE], F32, name=f"first{c}", tag=f"first{c}") for c in range(len(ranges))]
+        first = keep.tile([P, T], F32, name="first")
         turned = keep.tile([P, T], F32, name="turned")
         result = keep.tile([P, T], F32, name="result")
-        sums = [psum.tile([P, RANGE], F32, name=f"sum{c}", tag=f"bank{c}") for c in range(len(ranges))]
-        back = [psum.tile([P, RANGE], F32, name=f"back{c}", tag=f"bank{3 + c}") for c in range(len(ranges))]
+        sums = [psum.tile([P, RANGE], F32, name=f"sum{c}", tag=f"bank{3 + c}") for c in range(len(ranges))]
+        back = [psum.tile([P, RANGE], F32, name=f"back{c}", tag=f"bank{(6 + c) % 8}") for c in range(len(ranges))]
 
         def turn(bank, src, opens, closes):
             for at in range(0, RANGE, P):
@@ -178,26 +181,26 @@ def tile_moe_shr_lin_silu_kernel(tc, x_words, x_scales, w, b, gate, offs, pos1, 
             turn(back[c], turned[:, lo:hi], True, True)
 
         for c, (lo, hi) in enumerate(ranges):
-            fetch(first[c][:], pos1_sb, 0, lo, hi)
+            if c < 2:
+                end = hi if c == 0 else T
+                fetch(first[:, lo:end], pos1_sb, 0, lo, end)
             turn(sums[c], ys[:, lo:hi], True, False)
-            turn(sums[c], first[c], False, True)
+            turn(sums[c], first[:, lo:hi], False, True)
             nc.scalar.copy(turned[:, lo:hi], sums[c][:])
             if c > 0:
                 turn_back(c - 1)
         turn_back(len(ranges) - 1)
 
-        second = keep.tile([P, 2 * RANGE], F32, name="second")
-        second_last = keep.tile([P, RANGE], F32, name="second_last", tag="first2")
+        second = keep.tile([P, T], F32, name="second")
 
         def finish(lo, hi, second_part):
             c, at = divmod(lo, RANGE)
             nc.vector.tensor_tensor(result[:, lo:hi], back[c][:, at : at + hi - lo], second_part, ADD)
             nc.sync.dma_start(out[:, lo:hi], result[:, lo:hi])
 
-        for lo, hi in ranges[:2]:
+        for lo, hi in ((0, 2 * RANGE), (2 * RANGE, T)):
             fetch(second[:, lo:hi], pos2_sb, 1, lo, hi)
-        finish(0, RANGE, second[:, 0:RANGE])
-        fetch(second_last[:], pos2_sb, 1, 2 * RANGE, T)
-        finish(RANGE, 2 * RANGE, second[:, RANGE : 2 * RANGE])
-        for at in range(0, RANGE, P):
-            finish(2 * RANGE + at, 2 * RANGE + at + P, second_last[:, at : at + P])
+        for lo, hi in ranges[:2]:
+            finish(lo, hi, second[:, lo:hi])
+        for lo in range(2 * RANGE, T, P):
+            finish(lo, lo + P, second[:, lo : lo + P])

@@ -157,50 +157,43 @@ def tile_moe_shr_lin_silu_kernel(tc, x_words, x_scales, w, b, gate, offs, pos1, 
             nc.scalar.activation(ys[:, lo:hi], bank[:], SILU, bias=b_sb[:, E : E + 1])
 
         first = keep.tile([P, T], F32, name="first")
+        second = keep.tile([P, T], F32, name="second")
         turned = keep.tile([P, T], F32, name="turned")
         result = keep.tile([P, T], F32, name="result")
-        sums = [psum.tile([P, RANGE], F32, name=f"sum{c}", tag=f"bank{3 + c}") for c in range(len(ranges))]
-        back = [psum.tile([P, RANGE], F32, name=f"back{c}", tag=f"bank{(6 + c) % 8}") for c in range(len(ranges))]
+        half = T // 2
+        ways_in = [(0, 2 * P)] + [(lo, lo + P) for lo in range(2 * P, T, P)]
+        ways_out = [(0, 2 * P), (2 * P, 4 * P), (4 * P, 5 * P), (5 * P, T)]
+        sums = [psum.tile([P, hi - lo], F32, name=f"sum{lo}", tag=f"bank{3 + c}") for c, (lo, hi) in enumerate(ways_in)]
+        back = [psum.tile([P, hi - lo], F32, name=f"back{lo}", tag=f"bank{c}") for c, (lo, hi) in enumerate(ways_out)]
 
-        def turn(bank, src, opens, closes):
-            for at in range(0, RANGE, P):
-                nc.tensor.matmul(
-                    bank[:, at : at + P],
-                    src[:, at : at + P],
-                    ident[:],
-                    start=opens and (closes or at == 0),
-                    stop=closes and (opens or at + P == RANGE),
-                    is_transpose=True,
-                )
+        def turn(dst, src, start, stop):
+            nc.tensor.matmul(dst, src, ident[:], start=start, stop=stop, is_transpose=True)
+
+        def turn_in(src, lo0, hi0, opens):
+            for c, (lo, hi) in enumerate(ways_in):
+                if lo0 <= lo < hi0:
+                    for at in range(lo, hi, P):
+                        turn(sums[c][:, at - lo : at - lo + P], src[:, at : at + P], opens and at == lo, not opens and at + P == hi)
+                    if not opens:
+                        nc.scalar.copy(turned[:, lo:hi], sums[c][:])
+
+        def turn_back(lo0, hi0):
+            for c, (lo, hi) in enumerate(ways_out):
+                for at in range(max(lo, lo0), min(hi, hi0), P):
+                    turn(back[c][:, at - lo : at - lo + P], turned[:, at : at + P], True, True)
 
         def fetch(dst, pos_sb, r, lo, hi):
-            nc.vector.tensor_tensor(dst, y[:].indirect(entries(pos_sb, lo, hi)), gate_sb[r][:, lo:hi], MULT)
+            nc.vector.tensor_tensor(dst[:, lo:hi], y[:].indirect(entries(pos_sb, lo, hi)), gate_sb[r][:, lo:hi], MULT)
 
-        def turn_back(c):
-            lo, hi = ranges[c]
-            turn(back[c], turned[:, lo:hi], True, True)
-
-        for c, (lo, hi) in enumerate(ranges):
-            if c < 2:
-                end = hi if c == 0 else T
-                fetch(first[:, lo:end], pos1_sb, 0, lo, end)
-            turn(sums[c], ys[:, lo:hi], True, False)
-            turn(sums[c], first[:, lo:hi], False, True)
-            nc.scalar.copy(turned[:, lo:hi], sums[c][:])
-            if c > 0:
-                turn_back(c - 1)
-        turn_back(len(ranges) - 1)
-
-        second = keep.tile([P, T], F32, name="second")
-
-        def finish(lo, hi, second_part):
-            c, at = divmod(lo, RANGE)
-            nc.vector.tensor_tensor(result[:, lo:hi], back[c][:, at : at + hi - lo], second_part, ADD)
+        fetch(first, pos1_sb, 0, 0, half)
+        fetch(first, pos1_sb, 0, half, T)
+        turn_in(ys, 0, 4 * P, True)
+        turn_in(first, 0, half, False)
+        turn_in(ys, 4 * P, T, True)
+        turn_in(first, half, T, False)
+        turn_back(0, T)
+        for lo, hi in ((0, 4 * P), (4 * P, T)):
+            fetch(second, pos2_sb, 1, lo, hi)
+        for c, (lo, hi) in enumerate(ways_out):
+            nc.vector.tensor_tensor(result[:, lo:hi], back[c][:], second[:, lo:hi], ADD)
             nc.sync.dma_start(out[:, lo:hi], result[:, lo:hi])
-
-        for lo, hi in ((0, 2 * RANGE), (2 * RANGE, T)):
-            fetch(second[:, lo:hi], pos2_sb, 1, lo, hi)
-        for lo, hi in ranges[:2]:
-            finish(lo, hi, second[:, lo:hi])
-        for lo in range(2 * RANGE, T, P):
-            finish(lo, lo + P, second[:, lo : lo + P])

@@ -23,8 +23,8 @@ PACK = 4
 QUADRANT = 32
 PER_COLUMN = 16
 PAIR = 2 * C
-SCALE_WINDOW = 2048
-WORD_WINDOW = 1024
+SCALE_WINDOW = 2052
+WORD_WINDOW = 1025
 RANGE = 256
 GROUPS = [(0, 4), (4, 2), (E, 1)]
 LOADS = [(0, 1), (1, 2), (3, 1), (4, 1), (5, 1), (E, 1)]
@@ -58,15 +58,13 @@ def tile_moe_shr_lin_silu_kernel(tc, x_words, x_scales, w, b, gate, offs, pos1, 
         nc.gpsimd.memset(token_scales[:, :T].bitcast(I32), 0)
         nc.sync.dma_start(offs_sb[:], offs)
         for q in range(P // QUADRANT):
-            queue = nc.sync if q < 2 else nc.scalar
-            queue.dma_start(
+            nc.sync.dma_start(
                 token_scales[QUADRANT * q : QUADRANT * q + PACK, :T].bitcast(I32),
                 x_scales[0, PACK * q : PACK * q + PACK, :].bitcast(I32),
             )
-        nc.sync.dma_start(pos1_sb[:], pos1)
         nc.gpsimd.memset(warm_in[:], 0.0)
-        nc.gpsimd.memset(token_scales[:, T:].bitcast(I32), 0)
-        nc.gpsimd.memset(token_words[:, T:], 0)
+        nc.vector.memset(token_scales[:, T:].bitcast(I32), 0)
+        nc.vector.memset(token_words[:, T:], 0)
         nc.scalar.activation(warm_out[:], warm_in[:], SILU)
         ident = keep.tile([P, P], F32, name="ident")
         nc.gpsimd.memset(ident[:], 0.0)
@@ -85,6 +83,7 @@ def tile_moe_shr_lin_silu_kernel(tc, x_words, x_scales, w, b, gate, offs, pos1, 
         for g in range(2, len(LOADS)):
             load_weights(g)
         nc.sync.dma_start(b_sb[:], b)
+        nc.sync.dma_start(pos1_sb[:], pos1)
         nc.sync.dma_start(pos2_sb[:], pos2)
         for r in range(2):
             nc.sync.dma_start(gate_sb[r][:], gate[r])

@@ -80,9 +80,9 @@ def tile_moe_shr_lin_silu_kernel(tc, x_words, x_scales, w, b, gate, offs, pos1, 
         load_weights(0)
         load_weights(1)
         nc.sync.dma_start(token_words[:, :T], x_words[0].rearrange("p t r -> p (t r)").bitcast(I32))
+        nc.sync.dma_start(b_sb[:], b)
         for g in range(2, len(LOADS)):
             load_weights(g)
-        nc.sync.dma_start(b_sb[:], b)
         nc.sync.dma_start(pos1_sb[:], pos1)
         nc.sync.dma_start(pos2_sb[:], pos2)
         for r in range(2):
@@ -156,12 +156,12 @@ def tile_moe_shr_lin_silu_kernel(tc, x_words, x_scales, w, b, gate, offs, pos1, 
             nc.scalar.activation(ys[:, lo:hi], bank[:], SILU, bias=b_sb[:, E : E + 1])
 
         first = keep.tile([P, T], F32, name="first")
-        second = keep.tile([P, T], F32, name="second")
-        turned = keep.tile([P, T], F32, name="turned")
+        second = keep.tile([P, T - P], F32, name="second")
         result = keep.tile([P, T], F32, name="result")
         half = T // 2
         ways_in = [(0, 2 * P)] + [(lo, lo + P) for lo in range(2 * P, T, P)]
         ways_out = [(0, 2 * P), (2 * P, 4 * P), (4 * P, 5 * P), (5 * P, T)]
+        turned = [keep.tile([P, hi - lo], F32, name=f"turned{lo}", tag=f"turned{lo}") for lo, hi in ways_out]
         sums = [psum.tile([P, hi - lo], F32, name=f"sum{lo}", tag=f"bank{3 + c}") for c, (lo, hi) in enumerate(ways_in)]
         back = [psum.tile([P, hi - lo], F32, name=f"back{lo}", tag=f"bank{c}") for c, (lo, hi) in enumerate(ways_out)]
 
@@ -174,25 +174,35 @@ def tile_moe_shr_lin_silu_kernel(tc, x_words, x_scales, w, b, gate, offs, pos1, 
                     for at in range(lo, hi, P):
                         turn(sums[c][:, at - lo : at - lo + P], src[:, at : at + P], opens and at == lo, not opens and at + P == hi)
                     if not opens:
-                        nc.scalar.copy(turned[:, lo:hi], sums[c][:])
+                        o = max(i for i, (start, end) in enumerate(ways_out) if start <= lo)
+                        nc.scalar.copy(turned[o][:, lo - ways_out[o][0] : hi - ways_out[o][0]], sums[c][:])
 
         def turn_back(lo0, hi0):
             for c, (lo, hi) in enumerate(ways_out):
                 for at in range(max(lo, lo0), min(hi, hi0), P):
-                    turn(back[c][:, at - lo : at - lo + P], turned[:, at : at + P], True, True)
+                    turn(back[c][:, at - lo : at - lo + P], turned[c][:, at - lo : at - lo + P], True, True)
 
         def fetch(dst, pos_sb, r, lo, hi):
-            nc.vector.tensor_tensor(dst[:, lo:hi], y[:].indirect(entries(pos_sb, lo, hi)), gate_sb[r][:, lo:hi], MULT)
+            nc.vector.tensor_tensor(dst, y[:].indirect(entries(pos_sb, lo, hi)), gate_sb[r][:, lo:hi], MULT)
 
-        fetch(first, pos1_sb, 0, 0, half)
-        fetch(first, pos1_sb, 0, half, T)
+        fetch(first[:, :half], pos1_sb, 0, 0, half)
+        fetch(first[:, half:], pos1_sb, 0, half, T)
         turn_in(ys, 0, 4 * P, True)
         turn_in(first, 0, half, False)
         turn_in(ys, 4 * P, T, True)
         turn_in(first, half, T, False)
         turn_back(0, T)
-        for lo, hi in ((0, 4 * P), (4 * P, T)):
-            fetch(second, pos2_sb, 1, lo, hi)
-        for c, (lo, hi) in enumerate(ways_out):
-            nc.vector.tensor_tensor(result[:, lo:hi], back[c][:], second[:, lo:hi], ADD)
+        second_last = keep.tile([P, P], F32, name="second_last", tag=f"turned{ways_out[1][0]}")
+
+        def finish(c, second_part):
+            lo, hi = ways_out[c]
+            nc.vector.tensor_tensor(result[:, lo:hi], back[c][:], second_part, ADD)
             nc.sync.dma_start(out[:, lo:hi], result[:, lo:hi])
+
+        for lo, hi in ((0, 2 * P), (2 * P, T - P)):
+            fetch(second[:, lo:hi], pos2_sb, 1, lo, hi)
+        for c in range(2):
+            finish(c, second[:, ways_out[c][0] : ways_out[c][1]])
+        fetch(second_last[:], pos2_sb, 1, T - P, T)
+        finish(2, second[:, 4 * P : 5 * P])
+        finish(3, second_last[:])

@@ -22,12 +22,13 @@ P = 128
 PACK = 4
 QUADRANT = 32
 PER_COLUMN = 16
-PAIR = 2 * C
-SCALE_WINDOW = 2052
-WORD_WINDOW = 1025
-RANGE = 256
-GROUPS = [(0, 4), (4, 2), (E, 1)]
+BANKS = 8
+SCALE_WINDOW = 4 * S // 3 + 4
+WORD_WINDOW = 4 * T // 3 + 1
 LOADS = [(0, 1), (1, 2), (3, 1), (4, 1), (5, 1), (E, 1)]
+GROUPS = [(0, 4), (4, 2), (E, 1)]
+WAYS_IN = [(0, 2 * P), (2 * P, 3 * P), (3 * P, 4 * P), (4 * P, 5 * P), (5 * P, T)]
+WAYS_OUT = [(0, 3 * P), (3 * P, 5 * P), (5 * P, T)]
 
 
 def tile_moe_shr_lin_silu_kernel(tc, x_words, x_scales, w, b, gate, offs, pos1, pos2, out):
@@ -70,30 +71,31 @@ def tile_moe_shr_lin_silu_kernel(tc, x_words, x_scales, w, b, gate, offs, pos1, 
         nc.gpsimd.memset(ident[:], 0.0)
         make_identity(nc, ident[:], nomemset=True)
 
-        def load_weights(g):
-            e, count = LOADS[g]
+        def load_weights(load):
+            e0, n = LOADS[load]
             nc.sync.dma_start(
-                w_raw[g][:].rearrange("p e j n -> p e (j n)"),
-                w[e : e + count].rearrange("e (p j) n -> p e (j n)", j=PACK),
+                w_raw[load][:].rearrange("p e j n -> p e (j n)"),
+                w[e0 : e0 + n].rearrange("e (p j) n -> p e (j n)", j=PACK),
             )
 
         load_weights(0)
         load_weights(1)
         nc.sync.dma_start(token_words[:, :T], x_words[0].rearrange("p t r -> p (t r)").bitcast(I32))
         nc.sync.dma_start(b_sb[:], b)
-        for g in range(2, len(LOADS)):
-            load_weights(g)
+        for load in range(2, len(LOADS)):
+            load_weights(load)
         nc.sync.dma_start(pos1_sb[:], pos1)
         nc.sync.dma_start(pos2_sb[:], pos2)
         for r in range(2):
             nc.sync.dma_start(gate_sb[r][:], gate[r])
 
-        group_of = {e0 + i: (g, i) for g, (e0, n) in enumerate(GROUPS) for i in range(n)}
-        for g, (e0, n) in enumerate(LOADS):
-            for i in range(n):
+        place_of = {e0 + i: (g, i) for g, (e0, n) in enumerate(GROUPS) for i in range(n)}
+        for load, (e0, n) in enumerate(LOADS):
+            for at in range(n):
+                g, i = place_of[e0 + at]
                 nc.scalar.copy(
-                    w_bf[group_of[e0 + i][0]][:, group_of[e0 + i][1]].rearrange("p (c i) j -> p c j i", i=4),
-                    w_raw[g][:, i].rearrange("p j (c i) -> p c j i", i=4),
+                    w_bf[g][:, i].rearrange("p (c m) j -> p c j m", m=4),
+                    w_raw[load][:, at].rearrange("p j (c m) -> p c j m", m=4),
                 )
 
         def quantize(g):
@@ -110,10 +112,14 @@ def tile_moe_shr_lin_silu_kernel(tc, x_words, x_scales, w, b, gate, offs, pos1, 
             window = token_words[:] if hi - lo >= T else token_words[:, :T]
             nc.vector.tensor_copy(dst, window.bitcast(U32).indirect(entries(offs_sb, lo, hi)))
 
-        def product(acc, e, words, scales):
-            g, i = group_of[e]
+        products = []
+
+        def expert(dst, e, words, scales):
+            g, i = place_of[e]
+            bank = psum.tile([P, dst.shape[1]], F32, name=f"product{len(products)}", tag=f"bank{len(products) % BANKS}")
+            products.append(bank)
             nc.tensor.matmul_mx(
-                out=acc,
+                out=bank[:],
                 lhsT=w_codes[g][:, i * N : (i + 1) * N].bitcast(FP8X4),
                 lhsT_scale=w_scales[g][:, i * N : (i + 1) * N],
                 rhs=words.bitcast(FP8X4),
@@ -121,18 +127,14 @@ def tile_moe_shr_lin_silu_kernel(tc, x_words, x_scales, w, b, gate, offs, pos1, 
                 start=True,
                 stop=True,
             )
+            nc.scalar.activation(dst, bank[:], SILU, bias=b_sb[:, e : e + 1])
 
         def routed(words, base, lo0, hi0):
-            cuts = sorted({lo0, hi0} | set(range(-(-lo0 // C) * C, hi0, C)))
+            cuts = [lo0] + [at for at in range(C, S, C) if lo0 < at < hi0] + [hi0]
             for lo, hi in zip(cuts, cuts[1:]):
-                e = lo // C
-                bank = psum.tile([P, hi - lo], F32, name=f"routed{lo}", tag=f"bank{len(used) % 8}")
-                used.append(lo)
-                product(bank[:], e, words[:, lo - base : hi - base], slot_scales[:, lo:hi])
-                nc.scalar.activation(y[:, lo:hi], bank[:], SILU, bias=b_sb[:, e : e + 1])
+                expert(y[:, lo:hi], lo // C, words[:, lo - base : hi - base], slot_scales[:, lo:hi])
 
-        used = []
-        words_a = keep.tile([P, 3 * C], U32, name="words_a", align_bytes=64)
+        words_a = keep.tile([P, 6 * P], U32, name="words_a", align_bytes=64)
         words_b = keep.tile([P, 3 * P], U32, name="words_b", tag="w_raw4", align_bytes=64)
         words_c = keep.tile([P, 3 * P], U32, name="words_c", tag="w_raw5", align_bytes=64)
 
@@ -141,68 +143,66 @@ def tile_moe_shr_lin_silu_kernel(tc, x_words, x_scales, w, b, gate, offs, pos1, 
         quantize(0)
         routed(words_a, 0, 0, 6 * P)
         gather_words(words_b[:], 6 * P, 9 * P)
-        routed(words_b, 6 * P, 6 * P, 8 * P)
+        routed(words_b, 6 * P, 6 * P, 4 * C)
         quantize(1)
-        routed(words_b, 6 * P, 8 * P, 9 * P)
+        routed(words_b, 6 * P, 4 * C, 9 * P)
         gather_words(words_c[:, : 2 * P], 9 * P, 11 * P)
         routed(words_c, 9 * P, 9 * P, 11 * P)
         gather_words(words_c[:, 2 * P :], 11 * P, S)
         routed(words_c, 9 * P, 11 * P, S)
         quantize(2)
-        ranges = [(lo, lo + RANGE) for lo in range(0, T, RANGE)]
-        for c, (lo, hi) in enumerate(ranges):
-            bank = psum.tile([P, RANGE], F32, name=f"shared{lo}", tag=f"bank{c}")
-            product(bank[:], E, token_words[:, lo:hi], token_scales[:, lo:hi])
-            nc.scalar.activation(ys[:, lo:hi], bank[:], SILU, bias=b_sb[:, E : E + 1])
+        for lo in range(0, T, C):
+            expert(ys[:, lo : lo + C], E, token_words[:, lo : lo + C], token_scales[:, lo : lo + C])
 
         first = keep.tile([P, T], F32, name="first")
         second = keep.tile([P, T - P], F32, name="second")
         result = keep.tile([P, T], F32, name="result")
-        half = T // 2
-        ways_in = [(0, 2 * P)] + [(lo, lo + P) for lo in range(2 * P, T, P)]
-        ways_out = [(0, 2 * P), (2 * P, 4 * P), (4 * P, 5 * P), (5 * P, T)]
-        turned = [keep.tile([P, hi - lo], F32, name=f"turned{lo}", tag=f"turned{lo}") for lo, hi in ways_out]
-        sums = [psum.tile([P, hi - lo], F32, name=f"sum{lo}", tag=f"bank{3 + c}") for c, (lo, hi) in enumerate(ways_in)]
-        back = [psum.tile([P, hi - lo], F32, name=f"back{lo}", tag=f"bank{c}") for c, (lo, hi) in enumerate(ways_out)]
+        turned = [keep.tile([P, hi - lo], F32, name=f"turned{lo}", tag=f"turned{lo}") for lo, hi in WAYS_OUT]
+        sums = [psum.tile([P, hi - lo], F32, name=f"sum{lo}", tag=f"bank{3 + c}") for c, (lo, hi) in enumerate(WAYS_IN)]
+        back = [psum.tile([P, hi - lo], F32, name=f"back{lo}", tag=f"bank{c}") for c, (lo, hi) in enumerate(WAYS_OUT)]
 
         def turn(dst, src, start, stop):
             nc.tensor.matmul(dst, src, ident[:], start=start, stop=stop, is_transpose=True)
 
-        def turn_in(src, lo0, hi0, opens):
-            for c, (lo, hi) in enumerate(ways_in):
+        def open_sums(lo0, hi0):
+            for c, (lo, hi) in enumerate(WAYS_IN):
                 if lo0 <= lo < hi0:
                     for at in range(lo, hi, P):
-                        turn(sums[c][:, at - lo : at - lo + P], src[:, at : at + P], opens and at == lo, not opens and at + P == hi)
-                    if not opens:
-                        o = max(i for i, (start, end) in enumerate(ways_out) if start <= lo)
-                        nc.scalar.copy(turned[o][:, lo - ways_out[o][0] : hi - ways_out[o][0]], sums[c][:])
+                        turn(sums[c][:, at - lo : at - lo + P], ys[:, at : at + P], at == lo, False)
 
-        def turn_back(lo0, hi0):
-            for c, (lo, hi) in enumerate(ways_out):
-                for at in range(max(lo, lo0), min(hi, hi0), P):
-                    turn(back[c][:, at - lo : at - lo + P], turned[c][:, at - lo : at - lo + P], True, True)
+        def close_sums(lo0, hi0):
+            for c, (lo, hi) in enumerate(WAYS_IN):
+                if lo0 <= lo < hi0:
+                    for at in range(lo, hi, P):
+                        turn(sums[c][:, at - lo : at - lo + P], first[:, at : at + P], False, at + P == hi)
+                    way = max(v for v, (start, end) in enumerate(WAYS_OUT) if start <= lo)
+                    base = WAYS_OUT[way][0]
+                    nc.scalar.copy(turned[way][:, lo - base : hi - base], sums[c][:])
 
         def fetch(dst, pos_sb, r, lo, hi):
             nc.vector.tensor_tensor(dst, y[:].indirect(entries(pos_sb, lo, hi)), gate_sb[r][:, lo:hi], MULT)
 
+        half = T // 2
         fetch(first[:, :half], pos1_sb, 0, 0, half)
         fetch(first[:, half:], pos1_sb, 0, half, T)
-        turn_in(ys, 0, 4 * P, True)
-        turn_in(first, 0, half, False)
-        turn_in(ys, 4 * P, T, True)
-        turn_in(first, half, T, False)
-        turn_back(0, T)
-        second_last = keep.tile([P, P], F32, name="second_last", tag=f"turned{ways_out[1][0]}")
+        open_sums(0, 2 * C)
+        close_sums(0, half)
+        open_sums(2 * C, T)
+        close_sums(half, T)
+        for way, (lo, hi) in enumerate(WAYS_OUT):
+            for at in range(0, hi - lo, P):
+                turn(back[way][:, at : at + P], turned[way][:, at : at + P], True, True)
 
-        def finish(c, second_part):
-            lo, hi = ways_out[c]
-            nc.vector.tensor_tensor(result[:, lo:hi], back[c][:], second_part, ADD)
+        second_last = keep.tile([P, P], F32, name="second_last", tag=f"turned{WAYS_OUT[0][0]}")
+
+        def finish(way, second_part):
+            lo, hi = WAYS_OUT[way]
+            nc.vector.tensor_tensor(result[:, lo:hi], back[way][:], second_part, ADD)
             nc.sync.dma_start(out[:, lo:hi], result[:, lo:hi])
 
-        for lo, hi in ((0, 2 * P), (2 * P, T - P)):
+        for lo, hi in WAYS_OUT[:2]:
             fetch(second[:, lo:hi], pos2_sb, 1, lo, hi)
-        for c in range(2):
-            finish(c, second[:, ways_out[c][0] : ways_out[c][1]])
-        fetch(second_last[:], pos2_sb, 1, T - P, T)
-        finish(2, second[:, 4 * P : 5 * P])
-        finish(3, second_last[:])
+        finish(0, second[:, slice(*WAYS_OUT[0])])
+        fetch(second_last[:], pos2_sb, 1, *WAYS_OUT[2])
+        finish(1, second[:, slice(*WAYS_OUT[1])])
+        finish(2, second_last[:])

@@ -59,10 +59,12 @@ def tile_moe_shr_lin_silu_kernel(tc, x_words, x_scales, w, b, gate, offs, pos1, 
         nc.gpsimd.memset(token_scales[:, :T].bitcast(I32), 0)
         nc.sync.dma_start(offs_sb[:], offs)
         for q in range(P // QUADRANT):
-            nc.sync.dma_start(
+            queue = nc.sync if q < 2 else nc.scalar
+            queue.dma_start(
                 token_scales[QUADRANT * q : QUADRANT * q + PACK, :T].bitcast(I32),
                 x_scales[0, PACK * q : PACK * q + PACK, :].bitcast(I32),
             )
+        nc.sync.dma_start(pos1_sb[:], pos1)
         nc.gpsimd.memset(warm_in[:], 0.0)
         nc.vector.memset(token_scales[:, T:].bitcast(I32), 0)
         nc.vector.memset(token_words[:, T:], 0)
@@ -84,7 +86,6 @@ def tile_moe_shr_lin_silu_kernel(tc, x_words, x_scales, w, b, gate, offs, pos1, 
         nc.sync.dma_start(b_sb[:], b)
         for load in range(2, len(LOADS)):
             load_weights(load)
-        nc.sync.dma_start(pos1_sb[:], pos1)
         nc.sync.dma_start(pos2_sb[:], pos2)
         for r in range(2):
             nc.sync.dma_start(gate_sb[r][:], gate[r])

@@ -22,6 +22,7 @@ P = 128
 PACK = 4
 QUADRANT = 32
 PER_COLUMN = 16
+FIRST_ROW = P - K // 32
 BANKS = 8
 SCALE_WINDOW = 4 * S // 3 + 4
 WORD_WINDOW = 4 * T // 3 + 1
@@ -41,29 +42,24 @@ def tile_moe_shr_lin_silu_kernel(tc, x_words, x_scales, w, b, gate, offs, pos1, 
         pos1_sb = keep.tile([P, T // PER_COLUMN], U16, name="pos1_sb")
         pos2_sb = keep.tile([P, T // PER_COLUMN], U16, name="pos2_sb")
         token_words = keep.tile([P, WORD_WINDOW], I32, name="token_words", align_bytes=64)
-        token_scales = keep.tile([P, SCALE_WINDOW], U8, name="token_scales", align_bytes=64)
+        token_scales = keep.tile([P, SCALE_WINDOW], U8, name="token_scales", tag="token_scales", align_bytes=64)
         warm_in = keep.tile([P, 1], F32, name="warm_in")
         warm_out = keep.tile([P, 1], F32, name="warm_out")
         b_sb = keep.tile([P, E + 1], F32, name="b_sb")
-        gate_sb = [keep.tile([P, T], F32, name=f"gate{r}") for r in range(2)]
         w_raw = [
             keep.tile([P, n, PACK, N], F32, name=f"w_raw{e0}", tag=f"w_raw{e0}", align_bytes=64) for e0, n in LOADS
         ]
         w_bf = [keep.tile([P, n, N, PACK], BF16, name=f"w_bf{e0}", align_bytes=64) for e0, n in GROUPS]
         w_codes = [keep.tile([P, n * N], U32, name=f"w_codes{e0}", align_bytes=64) for e0, n in GROUPS]
         w_scales = [keep.tile([P, n * N], U8, name=f"w_scales{e0}", align_bytes=64) for e0, n in GROUPS]
+        slot_rows = keep.tile([P, S], U8, name="slot_rows", align_bytes=64)
         slot_scales = keep.tile([P, S], U8, name="slot_scales", align_bytes=64)
         y = keep.tile([P, S], F32, name="y")
         ys = keep.tile([P, T], F32, name="ys")
 
-        nc.gpsimd.memset(token_scales[:, :T].bitcast(I32), 0)
         nc.sync.dma_start(offs_sb[:], offs)
-        for q in range(P // QUADRANT):
-            queue = nc.sync if q < 2 else nc.scalar
-            queue.dma_start(
-                token_scales[QUADRANT * q : QUADRANT * q + PACK, :T].bitcast(I32),
-                x_scales[0, PACK * q : PACK * q + PACK, :].bitcast(I32),
-            )
+        nc.sync.dma_start(token_scales[FIRST_ROW:, :T].bitcast(I32), x_scales[0].bitcast(I32))
+        nc.gpsimd.memset(token_scales[:FIRST_ROW, :T].bitcast(I32), 0)
         nc.sync.dma_start(pos1_sb[:], pos1)
         nc.gpsimd.memset(warm_in[:], 0.0)
         nc.vector.memset(token_scales[:, T:].bitcast(I32), 0)
@@ -72,6 +68,7 @@ def tile_moe_shr_lin_silu_kernel(tc, x_words, x_scales, w, b, gate, offs, pos1, 
         ident = keep.tile([P, P], F32, name="ident")
         nc.gpsimd.memset(ident[:], 0.0)
         make_identity(nc, ident[:], nomemset=True)
+        nc.gpsimd.memset(slot_scales[:].bitcast(I32), 0)
 
         def load_weights(load):
             e0, n = LOADS[load]
@@ -87,8 +84,6 @@ def tile_moe_shr_lin_silu_kernel(tc, x_words, x_scales, w, b, gate, offs, pos1, 
         for load in range(2, len(LOADS)):
             load_weights(load)
         nc.sync.dma_start(pos2_sb[:], pos2)
-        for r in range(2):
-            nc.sync.dma_start(gate_sb[r][:], gate[r])
 
         place_of = {e0 + i: (g, i) for g, (e0, n) in enumerate(GROUPS) for i in range(n)}
         for load, (e0, n) in enumerate(LOADS):
@@ -139,7 +134,21 @@ def tile_moe_shr_lin_silu_kernel(tc, x_words, x_scales, w, b, gate, offs, pos1, 
         words_b = keep.tile([P, 3 * P], U32, name="words_b", tag="w_raw4", align_bytes=64)
         words_c = keep.tile([P, 3 * P], U32, name="words_c", tag="w_raw5", align_bytes=64)
 
-        nc.vector.tensor_copy(slot_scales[:], token_scales[:].indirect(offs_sb[:]))
+        nc.vector.tensor_copy(slot_rows[:], token_scales[:].indirect(offs_sb[:]))
+        for q in range(P // QUADRANT):
+            nc.sync.dma_start(
+                slot_scales[QUADRANT * q : QUADRANT * q + PACK, :].bitcast(I32),
+                slot_rows[FIRST_ROW + PACK * q : FIRST_ROW + PACK * q + PACK, :].bitcast(I32),
+            )
+        gate_sb = keep.tile([P, 2, T], F32, name="gate_sb", tag="token_scales", align_bytes=64)
+        nc.sync.dma_start(gate_sb[:], gate.rearrange("r p t -> p r t"))
+        shared_scales = keep.tile([P, T], U8, name="shared_scales", tag="w_raw0", align_bytes=64)
+        nc.gpsimd.memset(shared_scales[:].bitcast(I32), 0)
+        for q in range(P // QUADRANT):
+            nc.sync.dma_start(
+                shared_scales[QUADRANT * q : QUADRANT * q + PACK, :].bitcast(I32),
+                x_scales[0, PACK * q : PACK * q + PACK, :].bitcast(I32),
+            )
         gather_words(words_a[:], 0, 6 * P)
         quantize(0)
         routed(words_a, 0, 0, 6 * P)
@@ -153,7 +162,7 @@ def tile_moe_shr_lin_silu_kernel(tc, x_words, x_scales, w, b, gate, offs, pos1, 
         routed(words_c, 9 * P, 11 * P, S)
         quantize(2)
         for lo in range(0, T, C):
-            expert(ys[:, lo : lo + C], E, token_words[:, lo : lo + C], token_scales[:, lo : lo + C])
+            expert(ys[:, lo : lo + C], E, token_words[:, lo : lo + C], shared_scales[:, lo : lo + C])
 
         first = keep.tile([P, T], F32, name="first")
         second = keep.tile([P, T - P], F32, name="second")
@@ -181,7 +190,7 @@ def tile_moe_shr_lin_silu_kernel(tc, x_words, x_scales, w, b, gate, offs, pos1, 
                     nc.scalar.copy(turned[way][:, lo - base : hi - base], sums[c][:])
 
         def fetch(dst, pos_sb, r, lo, hi):
-            nc.vector.tensor_tensor(dst, y[:].indirect(entries(pos_sb, lo, hi)), gate_sb[r][:, lo:hi], MULT)
+            nc.vector.tensor_tensor(dst, y[:].indirect(entries(pos_sb, lo, hi)), gate_sb[:, r, lo:hi], MULT)
 
         half = T // 2
         fetch(first[:, :half], pos1_sb, 0, 0, half)

@@ -26,7 +26,7 @@ FIRST_ROW = P - K // 32
 BANKS = 8
 SCALE_WINDOW = 4 * S // 3 + 4
 WORD_WINDOW = 4 * T // 3 + 1
-LOADS = [(0, 1), (1, 2), (3, 1), (4, 1), (5, 1), (E, 1)]
+LOADS = [(0, 3), (3, 1), (4, 1), (5, 1), (E, 1)]
 GROUPS = [(0, 4), (4, 2), (E, 1)]
 WAYS_IN = [(0, 2 * P), (2 * P, 3 * P), (3 * P, 4 * P), (4 * P, 5 * P), (5 * P, T)]
 WAYS_OUT = [(0, 3 * P), (3 * P, 5 * P), (5 * P, T)]
@@ -68,7 +68,6 @@ def tile_moe_shr_lin_silu_kernel(tc, x_words, x_scales, w, b, gate, offs, pos1, 
         ident = keep.tile([P, P], F32, name="ident")
         nc.gpsimd.memset(ident[:], 0.0)
         make_identity(nc, ident[:], nomemset=True)
-        nc.gpsimd.memset(slot_scales[:].bitcast(I32), 0)
 
         def load_weights(load):
             e0, n = LOADS[load]
@@ -78,10 +77,9 @@ def tile_moe_shr_lin_silu_kernel(tc, x_words, x_scales, w, b, gate, offs, pos1, 
             )
 
         load_weights(0)
-        load_weights(1)
         nc.sync.dma_start(token_words[:, :T], x_words[0].rearrange("p t r -> p (t r)").bitcast(I32))
         nc.sync.dma_start(b_sb[:], b)
-        for load in range(2, len(LOADS)):
+        for load in range(1, len(LOADS)):
             load_weights(load)
         nc.sync.dma_start(pos2_sb[:], pos2)
 
@@ -140,15 +138,16 @@ def tile_moe_shr_lin_silu_kernel(tc, x_words, x_scales, w, b, gate, offs, pos1, 
                 slot_scales[QUADRANT * q : QUADRANT * q + PACK, :].bitcast(I32),
                 slot_rows[FIRST_ROW + PACK * q : FIRST_ROW + PACK * q + PACK, :].bitcast(I32),
             )
-        gate_sb = keep.tile([P, 2, T], F32, name="gate_sb", tag="token_scales", align_bytes=64)
-        nc.sync.dma_start(gate_sb[:], gate.rearrange("r p t -> p r t"))
+        gate_sb = [keep.tile([P, T], F32, name="gate0", tag="token_scales", align_bytes=64)]
+        nc.sync.dma_start(gate_sb[0][:], gate[0])
         shared_scales = keep.tile([P, T], U8, name="shared_scales", tag="w_raw0", align_bytes=64)
-        nc.gpsimd.memset(shared_scales[:].bitcast(I32), 0)
         for q in range(P // QUADRANT):
             nc.sync.dma_start(
                 shared_scales[QUADRANT * q : QUADRANT * q + PACK, :].bitcast(I32),
                 x_scales[0, PACK * q : PACK * q + PACK, :].bitcast(I32),
             )
+        gate_sb.append(keep.tile([P, T], F32, name="gate1", tag="w_raw3", align_bytes=64))
+        nc.sync.dma_start(gate_sb[1][:], gate[1])
         gather_words(words_a[:], 0, 6 * P)
         quantize(0)
         routed(words_a, 0, 0, 6 * P)
@@ -190,7 +189,7 @@ def tile_moe_shr_lin_silu_kernel(tc, x_words, x_scales, w, b, gate, offs, pos1, 
                     nc.scalar.copy(turned[way][:, lo - base : hi - base], sums[c][:])
 
         def fetch(dst, pos_sb, r, lo, hi):
-            nc.vector.tensor_tensor(dst, y[:].indirect(entries(pos_sb, lo, hi)), gate_sb[:, r, lo:hi], MULT)
+            nc.vector.tensor_tensor(dst, y[:].indirect(entries(pos_sb, lo, hi)), gate_sb[r][:, lo:hi], MULT)
 
         half = T // 2
         fetch(first[:, :half], pos1_sb, 0, 0, half)

@@ -29,7 +29,7 @@ WORD_WINDOW = 4 * T // 3 + 1
 LOADS = [(0, 3), (3, 1), (4, 1), (5, 1), (E, 1)]
 GROUPS = [(0, 4), (4, 2), (E, 1)]
 WAYS_IN = [(0, 2 * P), (2 * P, 3 * P), (3 * P, 4 * P), (4 * P, 5 * P), (5 * P, T)]
-WAYS_OUT = [(0, 3 * P), (3 * P, 5 * P), (5 * P, T)]
+WAYS_OUT = [(0, 3 * P), (3 * P, T)]
 
 
 def tile_moe_shr_lin_silu_kernel(tc, x_words, x_scales, w, b, gate, offs, pos1, pos2, out):
@@ -138,16 +138,14 @@ def tile_moe_shr_lin_silu_kernel(tc, x_words, x_scales, w, b, gate, offs, pos1, 
                 slot_scales[QUADRANT * q : QUADRANT * q + PACK, :].bitcast(I32),
                 slot_rows[FIRST_ROW + PACK * q : FIRST_ROW + PACK * q + PACK, :].bitcast(I32),
             )
-        gate_sb = [keep.tile([P, T], F32, name="gate0", tag="token_scales", align_bytes=64)]
-        nc.sync.dma_start(gate_sb[0][:], gate[0])
+        gates = keep.tile([P, 2, T], F32, name="gates", tag="token_scales", align_bytes=64)
+        nc.sync.dma_start(gates[:], gate.rearrange("r p t -> p r t"))
         shared_scales = keep.tile([P, T], U8, name="shared_scales", tag="w_raw0", align_bytes=64)
         for q in range(P // QUADRANT):
             nc.sync.dma_start(
                 shared_scales[QUADRANT * q : QUADRANT * q + PACK, :].bitcast(I32),
                 x_scales[0, PACK * q : PACK * q + PACK, :].bitcast(I32),
             )
-        gate_sb.append(keep.tile([P, T], F32, name="gate1", tag="w_raw3", align_bytes=64))
-        nc.sync.dma_start(gate_sb[1][:], gate[1])
         gather_words(words_a[:], 0, 6 * P)
         quantize(0)
         routed(words_a, 0, 0, 6 * P)
@@ -164,7 +162,7 @@ def tile_moe_shr_lin_silu_kernel(tc, x_words, x_scales, w, b, gate, offs, pos1, 
             expert(ys[:, lo : lo + C], E, token_words[:, lo : lo + C], shared_scales[:, lo : lo + C])
 
         first = keep.tile([P, T], F32, name="first")
-        second = keep.tile([P, T - P], F32, name="second")
+        second = keep.tile([P, T], F32, name="second")
         result = keep.tile([P, T], F32, name="result")
         turned = [keep.tile([P, hi - lo], F32, name=f"turned{lo}", tag=f"turned{lo}") for lo, hi in WAYS_OUT]
         sums = [psum.tile([P, hi - lo], F32, name=f"sum{lo}", tag=f"bank{3 + c}") for c, (lo, hi) in enumerate(WAYS_IN)]
@@ -189,7 +187,7 @@ def tile_moe_shr_lin_silu_kernel(tc, x_words, x_scales, w, b, gate, offs, pos1, 
                     nc.scalar.copy(turned[way][:, lo - base : hi - base], sums[c][:])
 
         def fetch(dst, pos_sb, r, lo, hi):
-            nc.vector.tensor_tensor(dst, y[:].indirect(entries(pos_sb, lo, hi)), gate_sb[r][:, lo:hi], MULT)
+            nc.vector.tensor_tensor(dst, y[:].indirect(entries(pos_sb, lo, hi)), gates[:, r, lo:hi], MULT)
 
         half = T // 2
         fetch(first[:, :half], pos1_sb, 0, 0, half)
@@ -202,16 +200,9 @@ def tile_moe_shr_lin_silu_kernel(tc, x_words, x_scales, w, b, gate, offs, pos1, 
             for at in range(0, hi - lo, P):
                 turn(back[way][:, at : at + P], turned[way][:, at : at + P], True, True)
 
-        second_last = keep.tile([P, P], F32, name="second_last", tag=f"turned{WAYS_OUT[0][0]}")
-
-        def finish(way, second_part):
-            lo, hi = WAYS_OUT[way]
-            nc.vector.tensor_tensor(result[:, lo:hi], back[way][:], second_part, ADD)
+        fetch(second[:, :half], pos2_sb, 1, 0, half)
+        fetch(second[:, half:], pos2_sb, 1, half, T)
+        for lo in range(0, T, T // 4):
+            hi = lo + T // 4
+            nc.vector.tensor_tensor(result[:, lo:hi], back[lo // half][:, lo % half : lo % half + T // 4], second[:, lo:hi], ADD)
             nc.sync.dma_start(out[:, lo:hi], result[:, lo:hi])
-
-        for lo, hi in WAYS_OUT[:2]:
-            fetch(second[:, lo:hi], pos2_sb, 1, lo, hi)
-        finish(0, second[:, slice(*WAYS_OUT[0])])
-        fetch(second_last[:], pos2_sb, 1, *WAYS_OUT[2])
-        finish(1, second[:, slice(*WAYS_OUT[1])])
-        finish(2, second_last[:])

@@ -15,6 +15,7 @@ U16 = mybir.dt.uint16
 U8 = mybir.dt.uint8
 FP8X4 = mybir.dt.float8_e4m3fn_x4
 SILU = mybir.ActivationFunctionType.Silu
+COPY = mybir.ActivationFunctionType.Copy
 MULT = mybir.AluOpType.mult
 ADD = mybir.AluOpType.add
 
@@ -23,51 +24,43 @@ PACK = 4
 QUADRANT = 32
 PER_COLUMN = 16
 FIRST_ROW = P - K // 32
-BANKS = 8
-SCALE_WINDOW = 4 * S // 3 + 4
+EARLY = 2 * C
+SCALE_WINDOW = 4 * (S - EARLY) // 3 + 7
 WORD_WINDOW = 4 * T // 3 + 1
-LOADS = [(0, 3), (3, 1), (4, 1), (5, 1), (E, 1)]
-GROUPS = [(0, 4), (4, 2), (E, 1)]
-WAYS_IN = [(0, 2 * P), (2 * P, 3 * P), (3 * P, 4 * P), (4 * P, 5 * P), (5 * P, T)]
-WAYS_OUT = [(0, 3 * P), (3 * P, T)]
+LOADS = [(E, 1), (0, 2), (2, 1), (3, 1), (4, 1), (5, 1)]
+GROUPS = [(E, 1), (0, 2), (2, 3), (5, 1)]
+WAYS = [(P, 3 * P), (3 * P, 5 * P), (5 * P, T)]
 
 
 def tile_moe_shr_lin_silu_kernel(tc, x_words, x_scales, w, b, gate, offs, pos1, pos2, out):
     nc = tc.nc
     with ExitStack() as ctx:
         keep = ctx.enter_context(tc.tile_pool(name="keep", bufs=1))
+        placed = ctx.enter_context(tc.tile_pool(name="placed", bufs=1))
         psum = ctx.enter_context(tc.psum_pool(name="psum", bufs=1))
+
+        def bank(name, index, width):
+            return psum.tile([P, width], F32, name=name, tag=f"bank{index}")
 
         offs_sb = keep.tile([P, S // PER_COLUMN], U16, name="offs_sb")
         pos1_sb = keep.tile([P, T // PER_COLUMN], U16, name="pos1_sb")
         pos2_sb = keep.tile([P, T // PER_COLUMN], U16, name="pos2_sb")
-        token_words = keep.tile([P, WORD_WINDOW], I32, name="token_words", align_bytes=64)
+        token_words = keep.tile([P, WORD_WINDOW], I32, name="token_words", tag="token_words", align_bytes=64)
         token_scales = keep.tile([P, SCALE_WINDOW], U8, name="token_scales", tag="token_scales", align_bytes=64)
+        shared_scales = keep.tile([P, T], U8, name="shared_scales", align_bytes=64)
         warm_in = keep.tile([P, 1], F32, name="warm_in")
         warm_out = keep.tile([P, 1], F32, name="warm_out")
         b_sb = keep.tile([P, E + 1], F32, name="b_sb")
         w_raw = [
-            keep.tile([P, n, PACK, N], F32, name=f"w_raw{e0}", tag=f"w_raw{e0}", align_bytes=64) for e0, n in LOADS
+            keep.tile([P, n, PACK, N], F32, name=f"w_raw{e0}", tag=f"w_raw{e0}", align_bytes=64) for e0, n in LOADS[:-1]
         ]
+        w_raw.append(placed.tile([P, 1, PACK, N], F32, name="w_raw_last", offset=0, align_bytes=64))
         w_bf = [keep.tile([P, n, N, PACK], BF16, name=f"w_bf{e0}", align_bytes=64) for e0, n in GROUPS]
         w_codes = [keep.tile([P, n * N], U32, name=f"w_codes{e0}", align_bytes=64) for e0, n in GROUPS]
         w_scales = [keep.tile([P, n * N], U8, name=f"w_scales{e0}", align_bytes=64) for e0, n in GROUPS]
-        slot_rows = keep.tile([P, S], U8, name="slot_rows", align_bytes=64)
-        slot_scales = keep.tile([P, S], U8, name="slot_scales", align_bytes=64)
-        y = keep.tile([P, S], F32, name="y")
-        ys = keep.tile([P, T], F32, name="ys")
-
-        nc.sync.dma_start(offs_sb[:], offs)
-        nc.sync.dma_start(token_scales[FIRST_ROW:, :T].bitcast(I32), x_scales[0].bitcast(I32))
-        nc.gpsimd.memset(token_scales[:FIRST_ROW, :T].bitcast(I32), 0)
-        nc.sync.dma_start(pos1_sb[:], pos1)
-        nc.gpsimd.memset(warm_in[:], 0.0)
-        nc.vector.memset(token_scales[:, T:].bitcast(I32), 0)
-        nc.vector.memset(token_words[:, T:], 0)
-        nc.scalar.activation(warm_out[:], warm_in[:], SILU)
+        slot_rows = keep.tile([P, S - EARLY], U8, name="slot_rows", tag="slot_rows", align_bytes=64)
+        late_scales = keep.tile([P, S - EARLY], U8, name="late_scales", align_bytes=64)
         ident = keep.tile([P, P], F32, name="ident")
-        nc.gpsimd.memset(ident[:], 0.0)
-        make_identity(nc, ident[:], nomemset=True)
 
         def load_weights(load):
             e0, n = LOADS[load]
@@ -76,15 +69,35 @@ def tile_moe_shr_lin_silu_kernel(tc, x_words, x_scales, w, b, gate, offs, pos1, 
                 w[e0 : e0 + n].rearrange("e (p j) n -> p e (j n)", j=PACK),
             )
 
+        nc.sync.dma_start(offs_sb[:], offs)
+        nc.sync.dma_start(token_scales[FIRST_ROW:, :T].bitcast(I32), x_scales[0].bitcast(I32))
+        nc.gpsimd.memset(token_scales[:FIRST_ROW, :T].bitcast(I32), 0)
+        nc.gpsimd.memset(shared_scales[:].bitcast(I32), 0)
+        nc.gpsimd.memset(warm_in[:], 0.0)
+        nc.vector.memset(token_scales[:, T:].bitcast(I32), 0)
+        nc.vector.memset(token_words[:, T:], 0)
+        nc.scalar.activation(warm_out[:], warm_in[:], SILU)
+        nc.gpsimd.memset(ident[:], 0.0)
+        make_identity(nc, ident[:], nomemset=True)
+
         load_weights(0)
+        for q in range(P // QUADRANT):
+            nc.sync.dma_start(
+                shared_scales[QUADRANT * q : QUADRANT * q + PACK, :].bitcast(I32),
+                x_scales[0, PACK * q : PACK * q + PACK, :].bitcast(I32),
+            )
+        load_weights(1)
         nc.sync.dma_start(token_words[:, :T], x_words[0].rearrange("p t r -> p (t r)").bitcast(I32))
         nc.sync.dma_start(b_sb[:], b)
-        for load in range(1, len(LOADS)):
+        for load in range(2, len(LOADS)):
             load_weights(load)
+        nc.sync.dma_start(pos1_sb[:], pos1)
         nc.sync.dma_start(pos2_sb[:], pos2)
 
         place_of = {e0 + i: (g, i) for g, (e0, n) in enumerate(GROUPS) for i in range(n)}
-        for load, (e0, n) in enumerate(LOADS):
+
+        def round_weights(load):
+            e0, n = LOADS[load]
             for at in range(n):
                 g, i = place_of[e0 + at]
                 nc.scalar.copy(
@@ -106,14 +119,10 @@ def tile_moe_shr_lin_silu_kernel(tc, x_words, x_scales, w, b, gate, offs, pos1, 
             window = token_words[:] if hi - lo >= T else token_words[:, :T]
             nc.vector.tensor_copy(dst, window.bitcast(U32).indirect(entries(offs_sb, lo, hi)))
 
-        products = []
-
-        def expert(dst, e, words, scales):
+        def expert(dst, e, words, scales, into):
             g, i = place_of[e]
-            bank = psum.tile([P, dst.shape[1]], F32, name=f"product{len(products)}", tag=f"bank{len(products) % BANKS}")
-            products.append(bank)
             nc.tensor.matmul_mx(
-                out=bank[:],
+                out=into[:],
                 lhsT=w_codes[g][:, i * N : (i + 1) * N].bitcast(FP8X4),
                 lhsT_scale=w_scales[g][:, i * N : (i + 1) * N],
                 rhs=words.bitcast(FP8X4),
@@ -121,88 +130,114 @@ def tile_moe_shr_lin_silu_kernel(tc, x_words, x_scales, w, b, gate, offs, pos1, 
                 start=True,
                 stop=True,
             )
-            nc.scalar.activation(dst, bank[:], SILU, bias=b_sb[:, e : e + 1])
-
-        def routed(words, base, lo0, hi0):
-            cuts = [lo0] + [at for at in range(C, S, C) if lo0 < at < hi0] + [hi0]
-            for lo, hi in zip(cuts, cuts[1:]):
-                expert(y[:, lo:hi], lo // C, words[:, lo - base : hi - base], slot_scales[:, lo:hi])
-
-        words_a = keep.tile([P, 6 * P], U32, name="words_a", align_bytes=64)
-        words_b = keep.tile([P, 3 * P], U32, name="words_b", tag="w_raw4", align_bytes=64)
-        words_c = keep.tile([P, 3 * P], U32, name="words_c", tag="w_raw5", align_bytes=64)
-
-        nc.vector.tensor_copy(slot_rows[:], token_scales[:].indirect(offs_sb[:]))
-        for q in range(P // QUADRANT):
-            nc.sync.dma_start(
-                slot_scales[QUADRANT * q : QUADRANT * q + PACK, :].bitcast(I32),
-                slot_rows[FIRST_ROW + PACK * q : FIRST_ROW + PACK * q + PACK, :].bitcast(I32),
-            )
-        gates = keep.tile([P, 2, T], F32, name="gates", tag="token_scales", align_bytes=64)
-        nc.sync.dma_start(gates[:], gate.rearrange("r p t -> p r t"))
-        shared_scales = keep.tile([P, T], U8, name="shared_scales", tag="w_raw0", align_bytes=64)
-        for q in range(P // QUADRANT):
-            nc.sync.dma_start(
-                shared_scales[QUADRANT * q : QUADRANT * q + PACK, :].bitcast(I32),
-                x_scales[0, PACK * q : PACK * q + PACK, :].bitcast(I32),
-            )
-        gather_words(words_a[:], 0, 6 * P)
-        quantize(0)
-        routed(words_a, 0, 0, 6 * P)
-        gather_words(words_b[:], 6 * P, 9 * P)
-        routed(words_b, 6 * P, 6 * P, 4 * C)
-        quantize(1)
-        routed(words_b, 6 * P, 4 * C, 9 * P)
-        gather_words(words_c[:, : 2 * P], 9 * P, 11 * P)
-        routed(words_c, 9 * P, 9 * P, 11 * P)
-        gather_words(words_c[:, 2 * P :], 11 * P, S)
-        routed(words_c, 9 * P, 11 * P, S)
-        quantize(2)
-        for lo in range(0, T, C):
-            expert(ys[:, lo : lo + C], E, token_words[:, lo : lo + C], shared_scales[:, lo : lo + C])
-
-        first = keep.tile([P, T], F32, name="first")
-        second = keep.tile([P, T], F32, name="second")
-        result = keep.tile([P, T], F32, name="result")
-        turned = [keep.tile([P, hi - lo], F32, name=f"turned{lo}", tag=f"turned{lo}") for lo, hi in WAYS_OUT]
-        sums = [psum.tile([P, hi - lo], F32, name=f"sum{lo}", tag=f"bank{3 + c}") for c, (lo, hi) in enumerate(WAYS_IN)]
-        back = [psum.tile([P, hi - lo], F32, name=f"back{lo}", tag=f"bank{c}") for c, (lo, hi) in enumerate(WAYS_OUT)]
+            nc.scalar.activation(dst, into[:], SILU, bias=b_sb[:, e : e + 1])
 
         def turn(dst, src, start, stop):
             nc.tensor.matmul(dst, src, ident[:], start=start, stop=stop, is_transpose=True)
 
-        def open_sums(lo0, hi0):
-            for c, (lo, hi) in enumerate(WAYS_IN):
-                if lo0 <= lo < hi0:
-                    for at in range(lo, hi, P):
-                        turn(sums[c][:, at - lo : at - lo + P], ys[:, at : at + P], at == lo, False)
+        for load in range(3):
+            round_weights(load)
 
-        def close_sums(lo0, hi0):
-            for c, (lo, hi) in enumerate(WAYS_IN):
-                if lo0 <= lo < hi0:
-                    for at in range(lo, hi, P):
-                        turn(sums[c][:, at - lo : at - lo + P], first[:, at : at + P], False, at + P == hi)
-                    way = max(v for v, (start, end) in enumerate(WAYS_OUT) if start <= lo)
-                    base = WAYS_OUT[way][0]
-                    nc.scalar.copy(turned[way][:, lo - base : hi - base], sums[c][:])
+        nc.vector.tensor_copy(slot_rows[:], token_scales[:].indirect(entries(offs_sb, EARLY, S)))
+        for q in range(P // QUADRANT):
+            nc.sync.dma_start(
+                late_scales[QUADRANT * q : QUADRANT * q + PACK, :].bitcast(I32),
+                slot_rows[FIRST_ROW + PACK * q : FIRST_ROW + PACK * q + PACK, :].bitcast(I32),
+            )
+        gate0 = keep.tile([P, T], F32, name="gate0", tag="token_scales", align_bytes=64)
+        nc.sync.dma_start(gate0[:], gate[0])
+        gate1 = keep.tile([P, P], F32, name="gate1", tag="slot_rows", align_bytes=64)
+        nc.sync.dma_start(gate1[:], gate[1, :, :P])
 
-        def fetch(dst, pos_sb, r, lo, hi):
-            nc.vector.tensor_tensor(dst, y[:].indirect(entries(pos_sb, lo, hi)), gates[:, r, lo:hi], MULT)
+        quantize(0)
+        early_scales = keep.tile([P, EARLY], U8, name="early_scales", tag=f"w_raw{E}", align_bytes=64)
+        nc.vector.tensor_copy(early_scales[:], shared_scales[:].indirect(entries(offs_sb, 0, EARLY)))
+        ys = keep.tile([P, T], F32, name="ys", tag="w_raw2", align_bytes=64)
+        halves = [(0, 4 * P), (4 * P, T)]
+        ys_turned_banks = []
+        for h, (lo, hi) in enumerate(halves):
+            expert(ys[:, lo:hi], E, token_words[:, lo:hi], shared_scales[:, lo:hi], bank(f"shared{h}", h, hi - lo))
+        for load in range(3, len(LOADS)):
+            round_weights(load)
+        gate1_turned = keep.tile([P, T // P - 1], F32, name="gate1_turned", tag="w_raw3", align_bytes=64)
+        with nc.allow_non_contiguous_dma(reason="one weight a token, a token a partition"):
+            nc.sync.dma_start(gate1_turned[:], gate[1, 0, P:].rearrange("(c p) -> p c", p=P))
+        turned_halves = [(P, 5 * P), (5 * P, T)]
+        for h, (lo, hi) in enumerate(turned_halves):
+            into = bank(f"ys_turned{h}", 2 + h, hi - lo)
+            ys_turned_banks.append(into)
+            for at in range(lo, hi, P):
+                turn(into[:, at - lo : at - lo + P], ys[:, at : at + P], True, True)
 
-        half = T // 2
-        fetch(first[:, :half], pos1_sb, 0, 0, half)
-        fetch(first[:, half:], pos1_sb, 0, half, T)
-        open_sums(0, 2 * C)
-        close_sums(0, half)
-        open_sums(2 * C, T)
-        close_sums(half, T)
-        for way, (lo, hi) in enumerate(WAYS_OUT):
-            for at in range(0, hi - lo, P):
-                turn(back[way][:, at : at + P], turned[way][:, at : at + P], True, True)
+        y = placed.tile([P, S], F32, name="y", offset=4 * P, align_bytes=64)
+        product_banks = [4, 5, 6, 7, 0, 1, 4, 5]
+        pieces = []
 
-        fetch(second[:, :half], pos2_sb, 1, 0, half)
-        fetch(second[:, half:], pos2_sb, 1, half, T)
-        for lo in range(0, T, T // 4):
-            hi = lo + T // 4
-            nc.vector.tensor_tensor(result[:, lo:hi], back[lo // half][:, lo % half : lo % half + T // 4], second[:, lo:hi], ADD)
+        def routed(words, base, lo0, hi0):
+            cuts = [lo0] + [at for at in range(C, S, C) if lo0 < at < hi0] + [hi0]
+            for lo, hi in zip(cuts, cuts[1:]):
+                into = bank(f"product{lo}", product_banks[len(pieces)], hi - lo)
+                pieces.append(lo)
+                scales = early_scales[:, lo:hi] if lo < EARLY else late_scales[:, lo - EARLY : hi - EARLY]
+                expert(y[:, lo:hi], lo // C, words[:, lo - base : hi - base], scales, into)
+
+        words_a = keep.tile([P, 6 * P], U32, name="words_a", align_bytes=64)
+        words_b = keep.tile([P, 3 * P], U32, name="words_b", tag="w_raw0", align_bytes=64)
+        words_c = keep.tile([P, 2 * P], U32, name="words_c", tag="w_raw4", align_bytes=64)
+        words_d = placed.tile([P, P], U32, name="words_d", offset=0, align_bytes=64)
+        gather_words(words_a[:], 0, 6 * P)
+        quantize(1)
+        routed(words_a, 0, 0, 2 * C)
+        gather_words(words_b[:], 6 * P, 9 * P)
+        quantize(2)
+        routed(words_a, 0, 2 * C, 3 * C)
+        routed(words_b, 6 * P, 3 * C, 9 * P)
+        gather_words(words_c[:], 9 * P, 11 * P)
+        routed(words_c, 9 * P, 9 * P, 5 * C)
+        quantize(3)
+        routed(words_c, 9 * P, 5 * C, 11 * P)
+        gather_words(words_d[:], 11 * P, S)
+        routed(words_d, 11 * P, 11 * P, S)
+
+        ys_turned = keep.tile([P, T], F32, name="ys_turned", tag="token_words", align_bytes=64)
+        for h, (lo, hi) in enumerate(turned_halves):
+            nc.vector.tensor_copy(ys_turned[:, lo:hi], ys_turned_banks[h][:])
+
+        first = keep.tile([P, T], F32, name="first")
+        second = keep.tile([P, T], F32, name="second")
+        second_turned = keep.tile([P, T], F32, name="second_turned")
+        result = keep.tile([P, T], F32, name="result")
+        back = [bank(f"back{lo}", index, hi - lo) for index, (lo, hi) in zip([6, 7, 0], WAYS)]
+        ways_in = {at: bank(f"in{at}", at // P, P) for at in range(P, T, P)}
+        for way, (lo, hi) in enumerate(WAYS):
+            for at in range(lo, hi, P):
+                turn(back[way][:, at - lo : at - lo + P], ys_turned[:, at : at + P], at == lo, False)
+
+        for at in range(P, T, P):
+            nc.scalar.activation(second[:, at : at + P], y[:].indirect(entries(pos2_sb, at, at + P)), COPY)
+
+        def fetch(dst, pos_sb, gate_sb, lo, hi):
+            nc.vector.tensor_tensor(dst[:, lo:hi], y[:].indirect(entries(pos_sb, lo, hi)), gate_sb[:, lo:hi], MULT)
+
+        part = keep.tile([P, P], F32, name="part")
+        fetch(second, pos2_sb, gate1, 0, P)
+        fetch(first, pos1_sb, gate0, 0, 3 * P)
+        nc.vector.tensor_tensor(part[:], ys[:, :P], second[:, :P], ADD)
+        fetch(first, pos1_sb, gate0, 3 * P, T)
+        nc.vector.tensor_tensor(result[:, :P], part[:], first[:, :P], ADD)
+        nc.sync.dma_start(out[:, :P], result[:, :P])
+        for way, (lo, hi) in enumerate(WAYS):
+            for at in range(lo, hi, P):
+                turn(ways_in[at][:], second[:, at : at + P], True, True)
+        for way, (lo, hi) in enumerate(WAYS):
+            for at in range(lo, hi, P):
+                nc.scalar.activation(
+                    second_turned[:, at : at + P],
+                    ways_in[at][:],
+                    COPY,
+                    scale=gate1_turned[:, at // P - 1 : at // P],
+                )
+            for at in range(lo, hi, P):
+                turn(back[way][:, at - lo : at - lo + P], second_turned[:, at : at + P], False, at + P == hi)
+            nc.vector.tensor_tensor(result[:, lo:hi], back[way][:], first[:, lo:hi], ADD)
             nc.sync.dma_start(out[:, lo:hi], result[:, lo:hi])

@@ -29,7 +29,8 @@ SCALE_WINDOW = 4 * (S - EARLY) // 3 + 7
 WORD_WINDOW = 4 * T // 3 + 1
 LOADS = [(E, 1), (0, 2), (2, 1), (3, 1), (4, 1), (5, 1)]
 GROUPS = [(E, 1), (0, 2), (2, 3), (5, 1)]
-WAYS = [(P, 3 * P), (3 * P, 5 * P), (5 * P, T)]
+PLAIN = 2 * P
+WAYS = [(PLAIN, 4 * P), (4 * P, 5 * P), (5 * P, T)]
 
 
 def tile_moe_shr_lin_silu_kernel(tc, x_words, x_scales, w, b, gate, offs, pos1, pos2, out):
@@ -119,7 +120,7 @@ def tile_moe_shr_lin_silu_kernel(tc, x_words, x_scales, w, b, gate, offs, pos1, 
             window = token_words[:] if hi - lo >= T else token_words[:, :T]
             nc.vector.tensor_copy(dst, window.bitcast(U32).indirect(entries(offs_sb, lo, hi)))
 
-        def expert(dst, e, words, scales, into):
+        def product(e, words, scales, into):
             g, i = place_of[e]
             nc.tensor.matmul_mx(
                 out=into[:],
@@ -130,7 +131,13 @@ def tile_moe_shr_lin_silu_kernel(tc, x_words, x_scales, w, b, gate, offs, pos1, 
                 start=True,
                 stop=True,
             )
+
+        def silu(dst, e, into):
             nc.scalar.activation(dst, into[:], SILU, bias=b_sb[:, e : e + 1])
+
+        def expert(dst, e, words, scales, into):
+            product(e, words, scales, into)
+            silu(dst, e, into)
 
         def turn(dst, src, start, stop):
             nc.tensor.matmul(dst, src, ident[:], start=start, stop=stop, is_transpose=True)
@@ -146,28 +153,28 @@ def tile_moe_shr_lin_silu_kernel(tc, x_words, x_scales, w, b, gate, offs, pos1, 
             )
         gate0 = keep.tile([P, T], F32, name="gate0", tag="token_scales", align_bytes=64)
         nc.sync.dma_start(gate0[:], gate[0])
-        gate1 = keep.tile([P, P], F32, name="gate1", tag="slot_rows", align_bytes=64)
-        nc.sync.dma_start(gate1[:], gate[1, :, :P])
+        gate1 = keep.tile([P, PLAIN], F32, name="gate1", tag="slot_rows", align_bytes=64)
+        nc.sync.dma_start(gate1[:], gate[1, :, :PLAIN])
 
         quantize(0)
         early_scales = keep.tile([P, EARLY], U8, name="early_scales", tag=f"w_raw{E}", align_bytes=64)
         nc.vector.tensor_copy(early_scales[:], shared_scales[:].indirect(entries(offs_sb, 0, EARLY)))
-        ys = keep.tile([P, T], F32, name="ys", tag="w_raw2", align_bytes=64)
-        halves = [(0, 4 * P), (4 * P, T)]
+        ys = keep.tile([P, T - PLAIN], F32, name="ys", tag="w_raw2", align_bytes=64)
         ys_turned_banks = []
-        for h, (lo, hi) in enumerate(halves):
-            expert(ys[:, lo:hi], E, token_words[:, lo:hi], shared_scales[:, lo:hi], bank(f"shared{h}", h, hi - lo))
+        expert(ys[:], E, token_words[:, PLAIN:T], shared_scales[:, PLAIN:], bank("shared", 0, T - PLAIN))
+        late_shared = bank("late_shared", 3, PLAIN)
+        product(E, token_words[:, :PLAIN], shared_scales[:, :PLAIN], late_shared)
         for load in range(3, len(LOADS)):
             round_weights(load)
-        gate1_turned = keep.tile([P, T // P - 1], F32, name="gate1_turned", tag="w_raw3", align_bytes=64)
+        gate1_turned = keep.tile([P, (T - PLAIN) // P], F32, name="gate1_turned", tag="w_raw3", align_bytes=64)
         with nc.allow_non_contiguous_dma(reason="one weight a token, a token a partition"):
-            nc.sync.dma_start(gate1_turned[:], gate[1, 0, P:].rearrange("(c p) -> p c", p=P))
-        turned_halves = [(P, 5 * P), (5 * P, T)]
+            nc.sync.dma_start(gate1_turned[:], gate[1, 0, PLAIN:].rearrange("(c p) -> p c", p=P))
+        turned_halves = [(PLAIN, T)]
         for h, (lo, hi) in enumerate(turned_halves):
             into = bank(f"ys_turned{h}", 2 + h, hi - lo)
             ys_turned_banks.append(into)
             for at in range(lo, hi, P):
-                turn(into[:, at - lo : at - lo + P], ys[:, at : at + P], True, True)
+                turn(into[:, at - lo : at - lo + P], ys[:, at - PLAIN : at - PLAIN + P], True, True)
 
         y = placed.tile([P, S], F32, name="y", offset=4 * P, align_bytes=64)
         product_banks = [4, 5, 6, 7, 0, 1, 4, 5]
@@ -204,40 +211,40 @@ def tile_moe_shr_lin_silu_kernel(tc, x_words, x_scales, w, b, gate, offs, pos1, 
             nc.vector.tensor_copy(ys_turned[:, lo:hi], ys_turned_banks[h][:])
 
         first = keep.tile([P, T], F32, name="first")
-        second = keep.tile([P, T], F32, name="second")
+        second = keep.tile([P, PLAIN], F32, name="second")
+        part = keep.tile([P, PLAIN], F32, name="part")
+        fetched = {at: keep.tile([P, P], F32, name=f"fetched{at}", tag=f"fetched{at}") for at in range(P, T, P)}
         second_turned = keep.tile([P, T], F32, name="second_turned")
         result = keep.tile([P, T], F32, name="result")
         back = [bank(f"back{lo}", index, hi - lo) for index, (lo, hi) in zip([6, 7, 0], WAYS)]
-        ways_in = {at: bank(f"in{at}", at // P, P) for at in range(P, T, P)}
+        ways_in = {at: bank(f"in{at}", index, P) for index, at in zip([1, 2, 4, 5], range(PLAIN, T, P))}
         for way, (lo, hi) in enumerate(WAYS):
             for at in range(lo, hi, P):
                 turn(back[way][:, at - lo : at - lo + P], ys_turned[:, at : at + P], at == lo, False)
 
         for at in range(P, T, P):
-            nc.scalar.activation(second[:, at : at + P], y[:].indirect(entries(pos2_sb, at, at + P)), COPY)
+            nc.scalar.activation(fetched[at][:], y[:].indirect(entries(pos2_sb, at, at + P)), COPY)
 
         def fetch(dst, pos_sb, gate_sb, lo, hi):
             nc.vector.tensor_tensor(dst[:, lo:hi], y[:].indirect(entries(pos_sb, lo, hi)), gate_sb[:, lo:hi], MULT)
 
-        part = keep.tile([P, P], F32, name="part")
+        fetch(first, pos1_sb, gate0, 0, PLAIN)
         fetch(second, pos2_sb, gate1, 0, P)
-        fetch(first, pos1_sb, gate0, 0, 3 * P)
-        nc.vector.tensor_tensor(part[:], ys[:, :P], second[:, :P], ADD)
-        fetch(first, pos1_sb, gate0, 3 * P, T)
-        nc.vector.tensor_tensor(result[:, :P], part[:], first[:, :P], ADD)
-        nc.sync.dma_start(out[:, :P], result[:, :P])
+        nc.vector.tensor_tensor(second[:, P:PLAIN], fetched[P][:], gate1[:, P:PLAIN], MULT)
+        fetch(first, pos1_sb, gate0, PLAIN, T)
+        nc.vector.tensor_tensor(part[:], first[:, :PLAIN], second[:], ADD)
+        for at in range(PLAIN, T, P):
+            turn(ways_in[at][:], fetched[at][:], True, True)
         for way, (lo, hi) in enumerate(WAYS):
             for at in range(lo, hi, P):
-                turn(ways_in[at][:], second[:, at : at + P], True, True)
-        for way, (lo, hi) in enumerate(WAYS):
-            for at in range(lo, hi, P):
-                nc.scalar.activation(
-                    second_turned[:, at : at + P],
-                    ways_in[at][:],
-                    COPY,
-                    scale=gate1_turned[:, at // P - 1 : at // P],
-                )
+                c = (at - PLAIN) // P
+                nc.scalar.activation(second_turned[:, at : at + P], ways_in[at][:], COPY, scale=gate1_turned[:, c : c + 1])
             for at in range(lo, hi, P):
                 turn(back[way][:, at - lo : at - lo + P], second_turned[:, at : at + P], False, at + P == hi)
             nc.vector.tensor_tensor(result[:, lo:hi], back[way][:], first[:, lo:hi], ADD)
             nc.sync.dma_start(out[:, lo:hi], result[:, lo:hi])
+            if way == 1:
+                ys_plain = keep.tile([P, PLAIN], F32, name="ys_plain", tag=f"fetched{T - 2 * P}")
+                silu(ys_plain[:], E, late_shared)
+                nc.vector.tensor_tensor(result[:, :PLAIN], part[:], ys_plain[:], ADD)
+                nc.sync.dma_start(out[:, :PLAIN], result[:, :PLAIN])

@@ -28,6 +28,7 @@ EARLY = 2 * C
 SCALE_WINDOW = 4 * (S - EARLY) // 3 + 7
 WORD_WINDOW = 4 * T // 3 + 1
 LOADS = [(E, 1), (0, 2), (2, 1), (3, 1), (4, 1), (5, 1)]
+ALIGN = 256
 GROUPS = [(E, 1), (0, 2), (2, 3), (5, 1)]
 PLAIN = 2 * P
 WAYS = [(PLAIN, 4 * P), (4 * P, 5 * P), (5 * P, T)]
@@ -43,25 +44,25 @@ def tile_moe_shr_lin_silu_kernel(tc, x_words, x_scales, w, b, gate, offs, pos1, 
         def bank(name, index, width):
             return psum.tile([P, width], F32, name=name, tag=f"bank{index}")
 
-        offs_sb = keep.tile([P, S // PER_COLUMN], U16, name="offs_sb")
+        offs_sb = keep.tile([P, S // PER_COLUMN], U16, name="offs_sb", align_bytes=ALIGN)
         pos1_sb = keep.tile([P, T // PER_COLUMN], U16, name="pos1_sb")
         pos2_sb = keep.tile([P, T // PER_COLUMN], U16, name="pos2_sb")
-        token_words = keep.tile([P, WORD_WINDOW], I32, name="token_words", tag="token_words", align_bytes=64)
-        token_scales = keep.tile([P, SCALE_WINDOW], U8, name="token_scales", tag="token_scales", align_bytes=64)
-        shared_scales = keep.tile([P, T], U8, name="shared_scales", align_bytes=64)
+        token_words = keep.tile([P, WORD_WINDOW], I32, name="token_words", tag="token_words", align_bytes=ALIGN)
+        token_scales = keep.tile([P, SCALE_WINDOW], U8, name="token_scales", tag="token_scales", align_bytes=ALIGN)
+        shared_scales = keep.tile([P, T], U8, name="shared_scales", align_bytes=ALIGN)
         warm_in = keep.tile([P, 1], F32, name="warm_in")
         warm_out = keep.tile([P, 1], F32, name="warm_out")
         b_sb = keep.tile([P, E + 1], F32, name="b_sb")
         w_raw = [
-            keep.tile([P, n, PACK, N], F32, name=f"w_raw{e0}", tag=f"w_raw{e0}", align_bytes=64) for e0, n in LOADS[:-1]
+            keep.tile([P, n, PACK, N], F32, name=f"w_raw{e0}", tag=f"w_raw{e0}", align_bytes=ALIGN) for e0, n in LOADS[:-1]
         ]
-        w_raw.append(placed.tile([P, 1, PACK, N], F32, name="w_raw_last", offset=0, align_bytes=64))
-        w_bf = [keep.tile([P, n, N, PACK], BF16, name=f"w_bf{e0}", align_bytes=64) for e0, n in GROUPS]
-        w_codes = [keep.tile([P, n * N], U32, name=f"w_codes{e0}", align_bytes=64) for e0, n in GROUPS]
-        w_scales = [keep.tile([P, n * N], U8, name=f"w_scales{e0}", align_bytes=64) for e0, n in GROUPS]
-        slot_rows = keep.tile([P, S - EARLY], U8, name="slot_rows", tag="slot_rows", align_bytes=64)
-        late_scales = keep.tile([P, S - EARLY], U8, name="late_scales", align_bytes=64)
-        ident = keep.tile([P, P], F32, name="ident")
+        w_raw.append(placed.tile([P, 1, PACK, N], F32, name="w_raw_last", offset=0, align_bytes=ALIGN))
+        w_bf = [keep.tile([P, n, N, PACK], BF16, name=f"w_bf{e0}", align_bytes=ALIGN) for e0, n in GROUPS]
+        w_codes = [keep.tile([P, n * N], U32, name=f"w_codes{e0}", align_bytes=ALIGN) for e0, n in GROUPS]
+        w_scales = [keep.tile([P, n * N], U8, name=f"w_scales{e0}", align_bytes=ALIGN) for e0, n in GROUPS]
+        slot_rows = keep.tile([P, S - EARLY], U8, name="slot_rows", tag="slot_rows", align_bytes=ALIGN)
+        late_scales = keep.tile([P, S - EARLY], U8, name="late_scales", align_bytes=ALIGN)
+        ident = keep.tile([P, P], F32, name="ident", align_bytes=ALIGN)
 
         def load_weights(load):
             e0, n = LOADS[load]
@@ -151,22 +152,22 @@ def tile_moe_shr_lin_silu_kernel(tc, x_words, x_scales, w, b, gate, offs, pos1, 
                 late_scales[QUADRANT * q : QUADRANT * q + PACK, :].bitcast(I32),
                 slot_rows[FIRST_ROW + PACK * q : FIRST_ROW + PACK * q + PACK, :].bitcast(I32),
             )
-        gate0 = keep.tile([P, T], F32, name="gate0", tag="token_scales", align_bytes=64)
+        gate0 = keep.tile([P, T], F32, name="gate0", tag="token_scales", align_bytes=ALIGN)
         nc.sync.dma_start(gate0[:], gate[0])
-        gate1 = keep.tile([P, PLAIN], F32, name="gate1", tag="slot_rows", align_bytes=64)
+        gate1 = keep.tile([P, PLAIN], F32, name="gate1", tag="slot_rows", align_bytes=ALIGN)
         nc.sync.dma_start(gate1[:], gate[1, :, :PLAIN])
 
         quantize(0)
-        early_scales = keep.tile([P, EARLY], U8, name="early_scales", tag=f"w_raw{E}", align_bytes=64)
+        early_scales = keep.tile([P, EARLY], U8, name="early_scales", tag=f"w_raw{E}", align_bytes=ALIGN)
         nc.vector.tensor_copy(early_scales[:], shared_scales[:].indirect(entries(offs_sb, 0, EARLY)))
-        ys = keep.tile([P, T - PLAIN], F32, name="ys", tag="w_raw2", align_bytes=64)
+        ys = keep.tile([P, T - PLAIN], F32, name="ys", tag="w_raw2", align_bytes=ALIGN)
         ys_turned_banks = []
         expert(ys[:], E, token_words[:, PLAIN:T], shared_scales[:, PLAIN:], bank("shared", 0, T - PLAIN))
         late_shared = bank("late_shared", 3, PLAIN)
         product(E, token_words[:, :PLAIN], shared_scales[:, :PLAIN], late_shared)
         for load in range(3, len(LOADS)):
             round_weights(load)
-        gate1_turned = keep.tile([P, (T - PLAIN) // P], F32, name="gate1_turned", tag="w_raw3", align_bytes=64)
+        gate1_turned = keep.tile([P, (T - PLAIN) // P], F32, name="gate1_turned", tag="w_raw3", align_bytes=ALIGN)
         with nc.allow_non_contiguous_dma(reason="one weight a token, a token a partition"):
             nc.sync.dma_start(gate1_turned[:], gate[1, 0, PLAIN:].rearrange("(c p) -> p c", p=P))
         turned_halves = [(PLAIN, T)]
@@ -176,7 +177,7 @@ def tile_moe_shr_lin_silu_kernel(tc, x_words, x_scales, w, b, gate, offs, pos1, 
             for at in range(lo, hi, P):
                 turn(into[:, at - lo : at - lo + P], ys[:, at - PLAIN : at - PLAIN + P], True, True)
 
-        y = placed.tile([P, S], F32, name="y", offset=4 * P, align_bytes=64)
+        y = placed.tile([P, S], F32, name="y", offset=4 * P, align_bytes=ALIGN)
         product_banks = [4, 5, 6, 7, 0, 1, 4, 5]
         pieces = []
 
@@ -188,10 +189,10 @@ def tile_moe_shr_lin_silu_kernel(tc, x_words, x_scales, w, b, gate, offs, pos1, 
                 scales = early_scales[:, lo:hi] if lo < EARLY else late_scales[:, lo - EARLY : hi - EARLY]
                 expert(y[:, lo:hi], lo // C, words[:, lo - base : hi - base], scales, into)
 
-        words_a = keep.tile([P, 6 * P], U32, name="words_a", align_bytes=64)
-        words_b = keep.tile([P, 3 * P], U32, name="words_b", tag="w_raw0", align_bytes=64)
-        words_c = keep.tile([P, 2 * P], U32, name="words_c", tag="w_raw4", align_bytes=64)
-        words_d = placed.tile([P, P], U32, name="words_d", offset=0, align_bytes=64)
+        words_a = keep.tile([P, 6 * P], U32, name="words_a", align_bytes=ALIGN)
+        words_b = keep.tile([P, 3 * P], U32, name="words_b", tag="w_raw0", align_bytes=ALIGN)
+        words_c = keep.tile([P, 2 * P], U32, name="words_c", tag="w_raw4", align_bytes=ALIGN)
+        words_d = placed.tile([P, P], U32, name="words_d", offset=0, align_bytes=ALIGN)
         gather_words(words_a[:], 0, 6 * P)
         quantize(1)
         routed(words_a, 0, 0, 2 * C)
@@ -206,16 +207,16 @@ def tile_moe_shr_lin_silu_kernel(tc, x_words, x_scales, w, b, gate, offs, pos1, 
         gather_words(words_d[:], 11 * P, S)
         routed(words_d, 11 * P, 11 * P, S)
 
-        ys_turned = keep.tile([P, T], F32, name="ys_turned", tag="token_words", align_bytes=64)
+        ys_turned = keep.tile([P, T], F32, name="ys_turned", tag="token_words", align_bytes=ALIGN)
         for h, (lo, hi) in enumerate(turned_halves):
             nc.vector.tensor_copy(ys_turned[:, lo:hi], ys_turned_banks[h][:])
 
-        first = keep.tile([P, T], F32, name="first")
+        first = keep.tile([P, T], F32, name="first", align_bytes=ALIGN)
         second = keep.tile([P, PLAIN], F32, name="second")
         part = keep.tile([P, PLAIN], F32, name="part")
         fetched = {at: keep.tile([P, P], F32, name=f"fetched{at}", tag=f"fetched{at}") for at in range(P, T, P)}
-        second_turned = keep.tile([P, T], F32, name="second_turned")
-        result = keep.tile([P, T], F32, name="result")
+        second_turned = keep.tile([P, T], F32, name="second_turned", align_bytes=ALIGN)
+        result = keep.tile([P, T], F32, name="result", align_bytes=ALIGN)
         back = [bank(f"back{lo}", index, hi - lo) for index, (lo, hi) in zip([6, 7, 0], WAYS)]
         ways_in = {at: bank(f"in{at}", index, P) for index, at in zip([1, 2, 4, 5], range(PLAIN, T, P))}
         for way, (lo, hi) in enumerate(WAYS):

from contextlib import ExitStack

import concourse.mybir as mybir
from concourse.masks import make_identity

K, T, E, C, N = 512, 768, 6, 256, 128
S = E * C
FLOPS = 2 * K * N * (S + T)

F32 = mybir.dt.float32
BF16 = mybir.dt.bfloat16
I32 = mybir.dt.int32
U32 = mybir.dt.uint32
U16 = mybir.dt.uint16
U8 = mybir.dt.uint8
FP8X4 = mybir.dt.float8_e4m3fn_x4
SILU = mybir.ActivationFunctionType.Silu
COPY = mybir.ActivationFunctionType.Copy
MULT = mybir.AluOpType.mult
ADD = mybir.AluOpType.add

P = 128
PACK = 4
QUADRANT = 32
PER_COLUMN = 16
FIRST_ROW = P - K // 32
EARLY = 2 * C
SCALE_WINDOW = 4 * (S - EARLY) // 3 + 7
WORD_WINDOW = 4 * T // 3 + 1
LOADS = [(E, 1), (0, 2), (2, 1), (3, 1), (4, 1), (5, 1)]
ALIGN = 256
GROUPS = [(E, 1), (0, 2), (2, 3), (5, 1)]
PLAIN = 2 * P
WAYS = [(PLAIN, 4 * P), (4 * P, 5 * P), (5 * P, T)]


def tile_moe_shr_lin_silu_kernel(tc, x_words, x_scales, w, b, gate, offs, pos1, pos2, out):
    nc = tc.nc
    with ExitStack() as ctx:
        keep = ctx.enter_context(tc.tile_pool(name="keep", bufs=1))
        placed = ctx.enter_context(tc.tile_pool(name="placed", bufs=1))
        psum = ctx.enter_context(tc.psum_pool(name="psum", bufs=1))

        def bank(name, index, width):
            return psum.tile([P, width], F32, name=name, tag=f"bank{index}")

        offs_sb = keep.tile([P, S // PER_COLUMN], U16, name="offs_sb", align_bytes=ALIGN)
        pos1_sb = keep.tile([P, T // PER_COLUMN], U16, name="pos1_sb")
        pos2_sb = keep.tile([P, T // PER_COLUMN], U16, name="pos2_sb")
        token_words = keep.tile([P, WORD_WINDOW], I32, name="token_words", tag="token_words", align_bytes=ALIGN)
        token_scales = keep.tile([P, SCALE_WINDOW], U8, name="token_scales", tag="token_scales", align_bytes=ALIGN)
        shared_scales = keep.tile([P, T], U8, name="shared_scales", align_bytes=ALIGN)
        warm_in = keep.tile([P, 1], F32, name="warm_in")
        warm_out = keep.tile([P, 1], F32, name="warm_out")
        b_sb = keep.tile([P, E + 1], F32, name="b_sb")
        w_raw = [
            keep.tile([P, n, PACK, N], F32, name=f"w_raw{e0}", tag=f"w_raw{e0}", align_bytes=ALIGN) for e0, n in LOADS[:-1]
        ]
        w_raw.append(placed.tile([P, 1, PACK, N], F32, name="w_raw_last", offset=0, align_bytes=ALIGN))
        w_bf = [keep.tile([P, n, N, PACK], BF16, name=f"w_bf{e0}", align_bytes=ALIGN) for e0, n in GROUPS]
        w_codes = [keep.tile([P, n * N], U32, name=f"w_codes{e0}", align_bytes=ALIGN) for e0, n in GROUPS]
        w_scales = [keep.tile([P, n * N], U8, name=f"w_scales{e0}", align_bytes=ALIGN) for e0, n in GROUPS]
        slot_rows = keep.tile([P, S - EARLY], U8, name="slot_rows", tag="slot_rows", align_bytes=ALIGN)
        late_scales = keep.tile([P, S - EARLY], U8, name="late_scales", align_bytes=ALIGN)
        ident = keep.tile([P, P], F32, name="ident", align_bytes=ALIGN)

        def load_weights(load):
            e0, n = LOADS[load]
            nc.sync.dma_start(
                w_raw[load][:].rearrange("p e j n -> p e (j n)"),
                w[e0 : e0 + n].rearrange("e (p j) n -> p e (j n)", j=PACK),
            )

        nc.sync.dma_start(offs_sb[:], offs)
        nc.sync.dma_start(token_scales[FIRST_ROW:, :T].bitcast(I32), x_scales[0].bitcast(I32))
        nc.gpsimd.memset(token_scales[:FIRST_ROW, :T].bitcast(I32), 0)
        nc.gpsimd.memset(shared_scales[:].bitcast(I32), 0)
        nc.gpsimd.memset(warm_in[:], 0.0)
        nc.vector.memset(token_scales[:, T:].bitcast(I32), 0)
        nc.vector.memset(token_words[:, T:], 0)
        nc.scalar.activation(warm_out[:], warm_in[:], SILU)
        nc.gpsimd.memset(ident[:], 0.0)
        make_identity(nc, ident[:], nomemset=True)

        load_weights(0)
        for q in range(P // QUADRANT):
            nc.sync.dma_start(
                shared_scales[QUADRANT * q : QUADRANT * q + PACK, :].bitcast(I32),
                x_scales[0, PACK * q : PACK * q + PACK, :].bitcast(I32),
            )
        load_weights(1)
        nc.sync.dma_start(token_words[:, :T], x_words[0].rearrange("p t r -> p (t r)").bitcast(I32))
        nc.sync.dma_start(b_sb[:], b)
        for load in range(2, len(LOADS)):
            load_weights(load)
        nc.sync.dma_start(pos1_sb[:], pos1)
        nc.sync.dma_start(pos2_sb[:], pos2)

        place_of = {e0 + i: (g, i) for g, (e0, n) in enumerate(GROUPS) for i in range(n)}

        def round_weights(load):
            e0, n = LOADS[load]
            for at in range(n):
                g, i = place_of[e0 + at]
                nc.scalar.copy(
                    w_bf[g][:, i].rearrange("p (c m) j -> p c j m", m=4),
                    w_raw[load][:, at].rearrange("p j (c m) -> p c j m", m=4),
                )

        def quantize(g):
            nc.vector.quantize_mx(
                out=w_codes[g][:].bitcast(FP8X4),
                scales=w_scales[g][:],
                in_=w_bf[g][:].rearrange("p e n j -> p (e n j)"),
            )

        def entries(list_sb, lo, hi):
            return list_sb[:, lo // PER_COLUMN : hi // PER_COLUMN]

        def gather_words(dst, lo, hi):
            window = token_words[:] if hi - lo >= T else token_words[:, :T]
            nc.vector.tensor_copy(dst, window.bitcast(U32).indirect(entries(offs_sb, lo, hi)))

        def product(e, words, scales, into):
            g, i = place_of[e]
            nc.tensor.matmul_mx(
                out=into[:],
                lhsT=w_codes[g][:, i * N : (i + 1) * N].bitcast(FP8X4),
                lhsT_scale=w_scales[g][:, i * N : (i + 1) * N],
                rhs=words.bitcast(FP8X4),
                rhs_scale=scales,
                start=True,
                stop=True,
            )

        def silu(dst, e, into):
            nc.scalar.activation(dst, into[:], SILU, bias=b_sb[:, e : e + 1])

        def expert(dst, e, words, scales, into):
            product(e, words, scales, into)
            silu(dst, e, into)

        def turn(dst, src, start, stop):
            nc.tensor.matmul(dst, src, ident[:], start=start, stop=stop, is_transpose=True)

        for load in range(3):
            round_weights(load)

        nc.vector.tensor_copy(slot_rows[:], token_scales[:].indirect(entries(offs_sb, EARLY, S)))
        for q in range(P // QUADRANT):
            nc.sync.dma_start(
                late_scales[QUADRANT * q : QUADRANT * q + PACK, :].bitcast(I32),
                slot_rows[FIRST_ROW + PACK * q : FIRST_ROW + PACK * q + PACK, :].bitcast(I32),
            )
        gate0 = keep.tile([P, T], F32, name="gate0", tag="token_scales", align_bytes=ALIGN)
        nc.sync.dma_start(gate0[:], gate[0])
        gate1 = keep.tile([P, PLAIN], F32, name="gate1", tag="slot_rows", align_bytes=ALIGN)
        nc.sync.dma_start(gate1[:], gate[1, :, :PLAIN])

        quantize(0)
        early_scales = keep.tile([P, EARLY], U8, name="early_scales", tag=f"w_raw{E}", align_bytes=ALIGN)
        nc.vector.tensor_copy(early_scales[:], shared_scales[:].indirect(entries(offs_sb, 0, EARLY)))
        ys = keep.tile([P, T - PLAIN], F32, name="ys", tag="w_raw2", align_bytes=ALIGN)
        ys_turned_banks = []
        expert(ys[:], E, token_words[:, PLAIN:T], shared_scales[:, PLAIN:], bank("shared", 0, T - PLAIN))
        late_shared = bank("late_shared", 3, PLAIN)
        product(E, token_words[:, :PLAIN], shared_scales[:, :PLAIN], late_shared)
        for load in range(3, len(LOADS)):
            round_weights(load)
        gate1_turned = keep.tile([P, (T - PLAIN) // P], F32, name="gate1_turned", tag="w_raw3", align_bytes=ALIGN)
        with nc.allow_non_contiguous_dma(reason="one weight a token, a token a partition"):
            nc.sync.dma_start(gate1_turned[:], gate[1, 0, PLAIN:].rearrange("(c p) -> p c", p=P))
        turned_halves = [(PLAIN, T)]
        for h, (lo, hi) in enumerate(turned_halves):
            into = bank(f"ys_turned{h}", 2 + h, hi - lo)
            ys_turned_banks.append(into)
            for at in range(lo, hi, P):
                turn(into[:, at - lo : at - lo + P], ys[:, at - PLAIN : at - PLAIN + P], True, True)

        y = placed.tile([P, S], F32, name="y", offset=4 * P, align_bytes=ALIGN)
        product_banks = [4, 5, 6, 7, 0, 1, 4, 5]
        pieces = []

        def routed(words, base, lo0, hi0):
            cuts = [lo0] + [at for at in range(C, S, C) if lo0 < at < hi0] + [hi0]
            for lo, hi in zip(cuts, cuts[1:]):
                into = bank(f"product{lo}", product_banks[len(pieces)], hi - lo)
                pieces.append(lo)
                scales = early_scales[:, lo:hi] if lo < EARLY else late_scales[:, lo - EARLY : hi - EARLY]
                expert(y[:, lo:hi], lo // C, words[:, lo - base : hi - base], scales, into)

        words_a = keep.tile([P, 6 * P], U32, name="words_a", align_bytes=ALIGN)
        words_b = keep.tile([P, 3 * P], U32, name="words_b", tag="w_raw0", align_bytes=ALIGN)
        words_c = keep.tile([P, 2 * P], U32, name="words_c", tag="w_raw4", align_bytes=ALIGN)
        words_d = placed.tile([P, P], U32, name="words_d", offset=0, align_bytes=ALIGN)
        gather_words(words_a[:], 0, 6 * P)
        quantize(1)
        routed(words_a, 0, 0, 2 * C)
        gather_words(words_b[:], 6 * P, 9 * P)
        quantize(2)
        routed(words_a, 0, 2 * C, 3 * C)
        routed(words_b, 6 * P, 3 * C, 9 * P)
        gather_words(words_c[:], 9 * P, 11 * P)
        routed(words_c, 9 * P, 9 * P, 5 * C)
        quantize(3)
        routed(words_c, 9 * P, 5 * C, 11 * P)
        gather_words(words_d[:], 11 * P, S)
        routed(words_d, 11 * P, 11 * P, S)

        ys_turned = keep.tile([P, T], F32, name="ys_turned", tag="token_words", align_bytes=ALIGN)
        for h, (lo, hi) in enumerate(turned_halves):
            nc.vector.tensor_copy(ys_turned[:, lo:hi], ys_turned_banks[h][:])

        first = keep.tile([P, T], F32, name="first", align_bytes=ALIGN)
        second = keep.tile([P, PLAIN], F32, name="second")
        part = keep.tile([P, PLAIN], F32, name="part")
        fetched = {at: keep.tile([P, P], F32, name=f"fetched{at}", tag=f"fetched{at}") for at in range(P, T, P)}
        second_turned = keep.tile([P, T], F32, name="second_turned", align_bytes=ALIGN)
        result = keep.tile([P, T], F32, name="result", align_bytes=ALIGN)
        back = [bank(f"back{lo}", index, hi - lo) for index, (lo, hi) in zip([6, 7, 0], WAYS)]
        ways_in = {at: bank(f"in{at}", index, P) for index, at in zip([1, 2, 4, 5], range(PLAIN, T, P))}
        for way, (lo, hi) in enumerate(WAYS):
            for at in range(lo, hi, P):
                turn(back[way][:, at - lo : at - lo + P], ys_turned[:, at : at + P], at == lo, False)

        for at in range(P, T, P):
            nc.scalar.activation(fetched[at][:], y[:].indirect(entries(pos2_sb, at, at + P)), COPY)

        def fetch(dst, pos_sb, gate_sb, lo, hi):
            nc.vector.tensor_tensor(dst[:, lo:hi], y[:].indirect(entries(pos_sb, lo, hi)), gate_sb[:, lo:hi], MULT)

        fetch(first, pos1_sb, gate0, 0, PLAIN)
        fetch(second, pos2_sb, gate1, 0, P)
        nc.vector.tensor_tensor(second[:, P:PLAIN], fetched[P][:], gate1[:, P:PLAIN], MULT)
        fetch(first, pos1_sb, gate0, PLAIN, T)
        nc.vector.tensor_tensor(part[:], first[:, :PLAIN], second[:], ADD)
        for at in range(PLAIN, T, P):
            turn(ways_in[at][:], fetched[at][:], True, True)
        for way, (lo, hi) in enumerate(WAYS):
            for at in range(lo, hi, P):
                c = (at - PLAIN) // P
                nc.scalar.activation(second_turned[:, at : at + P], ways_in[at][:], COPY, scale=gate1_turned[:, c : c + 1])
            for at in range(lo, hi, P):
                turn(back[way][:, at - lo : at - lo + P], second_turned[:, at : at + P], False, at + P == hi)
            nc.vector.tensor_tensor(result[:, lo:hi], back[way][:], first[:, lo:hi], ADD)
            nc.sync.dma_start(out[:, lo:hi], result[:, lo:hi])
            if way == 1:
                ys_plain = keep.tile([P, PLAIN], F32, name="ys_plain", tag=f"fetched{T - 2 * P}")
                silu(ys_plain[:], E, late_shared)
                nc.vector.tensor_tensor(result[:, :PLAIN], part[:], ys_plain[:], ADD)
                nc.sync.dma_start(out[:, :PLAIN], result[:, :PLAIN])
